import numpy as np
import ml_dtypes


def mxq(x, axis, fmt="e4m3"):
    dtype, down = {"e4m3": (ml_dtypes.float8_e4m3fn, 7), "e5m2": (ml_dtypes.float8_e5m2, 14)}[fmt]
    v = np.moveaxis(np.asarray(x, np.float32).astype(ml_dtypes.bfloat16).astype(np.float64), axis, -1)
    blocks = v.reshape(v.shape[:-1] + (-1, 32))
    amax = np.abs(blocks).max(-1, keepdims=True)
    byte = np.maximum(np.where(amax > 0, np.frexp(amax)[1] - 1 + 127, 0) - down, 1)
    scale = np.exp2(byte - 127.0)
    codes = (blocks / scale).astype(np.float32).astype(dtype).astype(np.float64)
    return np.moveaxis((codes * scale).reshape(v.shape), -1, axis)


WIDE = False


def mx_kscale(k):
    if not WIDE:
        return np.ones(k)
    levels = np.array([10, -10, 5, -5, 0])
    if k % 512:
        return np.exp2(np.random.permutation(np.resize(levels, k // 32))).repeat(32)
    a = np.empty((k // 512, 16))
    for p in range(k // 512):
        a[p, :8] = np.random.permutation(np.resize(levels, 8))
        for g in range(8):
            far = levels[np.abs(levels - a[p, g]) >= 10]
            a[p, g + 8] = far[np.random.randint(len(far))]
    return np.exp2(a.ravel()).repeat(32)


def f64(x):
    return np.asarray(x).astype(np.float64)


def striped(idx):
    return np.tile(idx.reshape(-1, 16).T, (8, 1)).astype(np.uint16)


def unstriped(offs):
    return offs[:16].T.reshape(-1).astype(np.int64)


E2M1 = np.array([0.0, 0.5, 1.0, 1.5, 2.0, 3.0, 4.0, 6.0, -0.0, -0.5, -1.0, -1.5, -2.0, -3.0, -4.0, -6.0])


def pack_weight(w, fmt):
    k, n = w.shape
    w = f64(np.asarray(w, np.float32).astype(ml_dtypes.bfloat16)).reshape(k // 32, 32, n)
    amax = np.abs(w).max(1)
    if fmt == "e4m3":
        byte = np.frexp(amax)[1] - 1 + 127 - 7
    else:
        mant, ex = np.frexp(amax / 6.0)
        byte = np.where(mant > 0.5, ex, ex - 1) + 127
    byte = np.clip(np.where(amax > 0, byte, 1), 1, 254)
    scaled = (w * np.exp2(127.0 - byte)[:, None, :]).reshape(k, n).astype(np.float32)
    by_word = np.ascontiguousarray(scaled.reshape(k // 512, 128, 4, n).transpose(0, 1, 3, 2))
    if fmt == "e4m3":
        words = by_word.astype(ml_dtypes.float8_e4m3fn).view(np.uint8)
    else:
        c = by_word.astype(ml_dtypes.float4_e2m1fn).view(np.uint8) & 0xF
        words = (c[..., 0::2] | (c[..., 1::2] << 4)).reshape(k // 512, 128, 2 * n)
    return np.ascontiguousarray(words), np.ascontiguousarray(byte.astype(np.uint8).reshape(k // 512, 16, n))


def unpack_weight(words, scales, fmt):
    g, _, n = scales.shape
    words = np.ascontiguousarray(words).reshape(g, 128, n, -1)
    if fmt == "e4m3":
        vals = words.view(ml_dtypes.float8_e4m3fn).astype(np.float64)
    else:
        nib = np.empty((g, 128, n, 4), np.uint8)
        nib[..., 0::2] = words & 0xF
        nib[..., 1::2] = words >> 4
        vals = E2M1[nib]
    vals = vals * np.repeat(np.exp2(scales.astype(np.float64) - 127.0), 8, axis=1)[..., None]
    return vals.transpose(0, 1, 3, 2).reshape(g * 512, n)


def gelu(v):
    return 0.5 * v * (1.0 + np.tanh(np.sqrt(2.0 / np.pi) * (v + 0.044715 * v**3)))


def bf(x):
    return np.asarray(x, np.float32).astype(ml_dtypes.bfloat16)

def planes(Y):
    n, m = Y.shape
    b = f64(bf(Y)).reshape(n // 32, 32, m)
    amax = np.abs(b).max(1)
    byte = np.clip(np.where(amax > 0, np.frexp(amax)[1] - 1 + 127 - 7, 1), 1, 254)
    codes = (b * np.exp2(127.0 - byte)[:, None, :]).reshape(n, m).astype(np.float32).astype(ml_dtypes.float8_e4m3fn).view(np.uint8)
    words = codes.reshape(n // 512, 128, 4, m).transpose(0, 1, 3, 2)
    return np.ascontiguousarray(words), np.ascontiguousarray(byte.astype(np.uint8).reshape(n // 512, 16, m))


K, T, S, H, N = 1024, 4096, 1024, 512, 512

def setup_inputs():
    n = np.random.standard_normal
    s = mx_kscale(K)[:, None]
    u = mx_kscale(H)[:, None]
    tab_words, tab_scales = pack_weight(n((K, T)) * s, "e4m3")
    w1 = n((K, H)) / np.sqrt(K) / s
    w4_words, w4_scales = pack_weight(-n((K, H)) / np.sqrt(K) / s, "e2m1")
    w8_words, w8_scales = pack_weight(n((K, H)) / np.sqrt(K) / s * u.T, "e4m3")
    wr = n((H, N)) / np.sqrt(H) * np.exp(0.8 * n(N)) / u
    return {"tab_words": tab_words, "tab_scales": tab_scales,
            "offs": striped(np.random.permutation(T)[:S]),
            "offs2": striped(np.random.permutation(T)[:S]),
            "offs3": striped(np.random.permutation(T)[:S]),
            "w1": w1.astype(np.float32),
            "w4_words": w4_words, "w4_scales": w4_scales,
            "w8_words": w8_words, "w8_scales": w8_scales,
            "wr": wr.astype(np.float32)}

def reference(tab_words, tab_scales, offs, offs2, offs3, w1, w4_words, w4_scales, w8_words, w8_scales, wr):
    rain = unpack_weight(tab_words, tab_scales, "e4m3")[:, unstriped(offs)]
    soil = unpack_weight(tab_words, tab_scales, "e4m3")[:, unstriped(offs2)]
    slope = unpack_weight(tab_words, tab_scales, "e4m3")[:, unstriped(offs3)]
    w4 = unpack_weight(w4_words, w4_scales, "e2m1")
    w8 = unpack_weight(w8_words, w8_scales, "e4m3")
    d = mxq(f64(w1), 0, "e4m3").T @ rain + w4.T @ soil
    g = w8.T @ slope
    h = np.log(1.0 + np.exp(d)) * g
    y = mxq(f64(wr), 0, "e4m3").T @ mxq(h, 0, "e4m3")
    words, scales = planes(y)
    return y, words, scales

@@ -1,0 +1,307 @@
+import math
+from contextlib import ExitStack
+
+import concourse.mybir as mybir
+
+K, T, S, H, N = 1024, 4096, 1024, 512, 512
+FLOPS = 2 * S * H * (3 * K + N)
+
+F32 = mybir.dt.float32
+BF16 = mybir.dt.bfloat16
+I32 = mybir.dt.int32
+U32 = mybir.dt.uint32
+U16 = mybir.dt.uint16
+U8 = mybir.dt.uint8
+E4M3 = mybir.dt.float8_e4m3fn_x4
+E2M1 = mybir.dt.float4_e2m1fn_x4
+ACT = mybir.ActivationFunctionType
+ALU = mybir.AluOpType
+
+P = 128
+PACK = 4
+PASSES = K // (P * PACK)
+QUADS = 4
+ROWS = 4
+CELLS = 128
+CHUNKS = S // CELLS
+HALF = S // 2
+FLOOR = 2.0 ** -60
+LOAD_WORDS = PASSES * (T + H // 2 + PACK * H + H + H // 2) + PACK * N
+
+
+def tile_list_runoff_routing_kernel(
+    tc, tab_words, tab_scales, offs, offs2, offs3, w1, w4_words, w4_scales, w8_words, w8_scales, wr,
+    out_0, out_1, out_2,
+):
+    nc = tc.nc
+    with ExitStack() as ctx:
+        keep = ctx.enter_context(tc.tile_pool(name="keep", bufs=1))
+        ring = ctx.enter_context(tc.tile_pool(name="ring", bufs=3))
+        loads = ctx.enter_context(tc.tile_pool(name="loads", bufs=1))
+        psum = ctx.enter_context(tc.psum_pool(name="psum", bufs=1))
+
+        def held(shape, dtype, name, tag=None):
+            return keep.tile(shape, dtype, name=name, tag=tag or name, align_bytes=64)
+
+        places = [0]
+
+        def landing(shape, dtype, name):
+            start = places[-1]
+            places.append(start + 4 * math.prod(shape[1:]))
+            return loads.tile(shape, dtype, name=name, offset=start)
+
+        tab_sc = held([P, T], U8, "tab_sc")
+        nc.vector.memset(tab_sc[:].bitcast(I32), 0)
+        one = loads.tile([P, LOAD_WORDS], F32, name="one", offset=0)
+        nc.vector.memset(one[:, 0:1], 1.0)
+        floor = held([P, 1], F32, "floor")
+        nc.vector.tensor_scalar_mul(floor[:], one[:, 0:1], FLOOR)
+        wsc_raw = [landing([P, PASSES * H // 4], I32, f"wsc_raw{k}") for k in range(2)]
+        soil_sc1 = held([P, S], U8, "soil_sc1")
+        nc.gpsimd.memset(soil_sc1[:].bitcast(I32), 0)
+        for plane in wsc_raw:
+            nc.gpsimd.memset(plane[:], 0)
+        warm = held([P, 1], F32, "warm")
+        nc.scalar.activation(warm[:], floor[:], ACT.Sigmoid)
+
+        lists = [held([P, S // 16], U16, f"list{i}") for i in range(3)]
+        for tile, src in zip(lists, (offs, offs2, offs3)):
+            nc.sync.dma_start(tile[:], src)
+        for a in range(PASSES):
+            for q in range(QUADS):
+                r0 = 32 * q + ROWS * a
+                nc.sync.dma_start(
+                    tab_sc[r0 : r0 + ROWS, :].bitcast(I32),
+                    tab_scales[a, ROWS * q : ROWS * (q + 1), :].bitcast(I32),
+                )
+        tab_w = [landing([P, T], I32, f"tab_w{a}") for a in range(PASSES)]
+
+        def load_tab(a):
+            nc.sync.dma_start(tab_w[a][:], tab_words[a].rearrange("p n i -> p (n i)").bitcast(I32))
+
+        w4_raw = landing([P, PASSES, H // 2], I32, "w4_raw")
+        nc.sync.dma_start(w4_raw[:], w4_words.bitcast(I32).rearrange("a p c -> p a c"))
+
+        def load_planes(plane, src):
+            for q in range(QUADS):
+                nc.sync.dma_start(
+                    plane[32 * q : 32 * q + ROWS, :].rearrange("r (a c) -> r a c", a=PASSES),
+                    src[:, ROWS * q : ROWS * (q + 1), :].bitcast(I32).rearrange("a r c -> r a c"),
+                )
+
+        load_planes(wsc_raw[0], w4_scales)
+        load_tab(0)
+        w1_raw = [landing([P, PACK, H], F32, f"w1_raw{a}") for a in range(PASSES)]
+        for a in range(PASSES):
+            nc.sync.dma_start(
+                w1_raw[a][:], w1[a * P * PACK : (a + 1) * P * PACK, :].rearrange("(p j) c -> p j c", j=PACK)
+            )
+        load_tab(1)
+        w8_raw = landing([P, PASSES, H], I32, "w8_raw")
+        nc.sync.dma_start(
+            w8_raw[:], w8_words.rearrange("a p c i -> a p (c i)").bitcast(I32).rearrange("a p c -> p a c")
+        )
+        wr_raw = landing([P, PACK, N], F32, "wr_raw")
+        wr_rows = wr.rearrange("(q t i) n -> t q i n", t=PACK, i=8)
+        for t in range(PACK):
+            nc.sync.dma_start(wr_raw[:, t, :], wr_rows[t])
+        load_planes(wsc_raw[1], w8_scales)
+
+        def gather(out, window, idx, lo, hi):
+            nc.vector.tensor_copy(out, window.indirect(lists[idx][:, lo // 16 : hi // 16]))
+
+        got_sc = [held([P, S], U8, f"got_sc{i}") for i in range(3)]
+        for i in (1, 0):
+            gather(got_sc[i][:], tab_sc[:], i, 0, S)
+        for q in range(QUADS):
+            nc.gpsimd.dma_start(
+                soil_sc1[32 * q : 32 * q + ROWS, :].bitcast(I32),
+                got_sc[1][32 * q + ROWS : 32 * q + 2 * ROWS, :].bitcast(I32),
+            )
+
+        w4_q = held([P, PASSES, H // 2], I32, "w4_q")
+        nc.vector.tensor_copy(
+            w4_q[:].rearrange("p a (t q i) -> p a t q i", t=PACK, i=4),
+            w4_raw[:].rearrange("p a (q t i) -> p a t q i", t=PACK, i=4),
+        )
+        wsc = [held([P, PASSES * H], U8, f"wsc{k}") for k in range(2)]
+
+        def deal_planes(k):
+            nc.vector.tensor_copy(
+                wsc[k][:].bitcast(I32).rearrange("p (a t q i) -> p a t q i", a=PASSES, t=PACK, i=2),
+                wsc_raw[k][:].rearrange("p (a q t i) -> p a t q i", a=PASSES, t=PACK, i=2),
+            )
+
+        deal_planes(0)
+        first = [held([P, S], U32, f"first{i}") for i in range(2)]
+        for i in (1, 0):
+            gather(first[i][:], tab_w[0][:].bitcast(U32), i, 0, S)
+        w1_q = [held([P, H], U32, f"w1_q{a}") for a in range(PASSES)]
+        w1_sc = [held([P, H], U8, f"w1_sc{a}") for a in range(PASSES)]
+        for a in range(PASSES):
+            grouped = held([P, H * PACK], BF16, f"w1_bf{a}")
+            dst = grouped[:].rearrange("p (t q u i j) -> p u t q j i", t=PACK, u=2, i=4, j=PACK)
+            src = w1_raw[a][:].rearrange("p j (q t u i) -> p u t q j i", t=PACK, u=2, i=4)
+            for u in range(2):
+                nc.scalar.copy(dst[:, u], src[:, u])
+            nc.vector.quantize_mx(w1_q[a][:].bitcast(E4M3), w1_sc[a][:], grouped[:])
+
+        gather(got_sc[2][:], tab_sc[:], 2, 0, S)
+        second = [[None, None] for i in range(2)]
+        for h in range(2):
+            for i in range(2):
+                tag = ("early", "late")[h] if i == 1 else None
+                second[i][h] = held([P, HALF], U32, f"second{i}{h}", tag)
+                gather(second[i][h][:], tab_w[1][:].bitcast(U32), i, h * HALF, (h + 1) * HALF)
+        slope1 = held([P, S], U32, "slope1")
+        gather(slope1[:], tab_w[1][:].bitcast(U32), 2, 0, S)
+
+        w8_q = held([P, PASSES, H], I32, "w8_q")
+        nc.vector.tensor_copy(
+            w8_q[:].rearrange("p a (t q i) -> p a t q i", t=PACK, i=8),
+            w8_raw[:].rearrange("p a (q t i) -> p a t q i", t=PACK, i=8),
+        )
+        deal_planes(1)
+
+        d_banks = [psum.tile([P, PACK, CELLS], F32, name=f"d{c}", tag=f"bank{c}") for c in range(CHUNKS)]
+
+        def w1_pass(a, c, words, cols, start, stop):
+            cells = slice(c * CELLS, (c + 1) * CELLS)
+            for t in range(PACK):
+                nc.tensor.matmul_mx(
+                    d_banks[c][:, t, :],
+                    lhsT=w1_q[a][:, t * P : (t + 1) * P].bitcast(E4M3),
+                    lhsT_scale=w1_sc[a][:, t * P : (t + 1) * P],
+                    rhs=words[:, cols].bitcast(E4M3),
+                    rhs_scale=got_sc[0][ROWS * a :, cells],
+                    start=start and t == 0,
+                    stop=stop and t == PACK - 1,
+                )
+
+        def w4_pass(a, c, words, cols, plane, start, stop):
+            cells = slice(c * CELLS, (c + 1) * CELLS)
+            for t in range(PACK):
+                nc.tensor.matmul_mx(
+                    d_banks[c][:, t, :],
+                    lhsT=w4_q[:, a, t * P // 2 : (t + 1) * P // 2].bitcast(U8).bitcast(E2M1),
+                    lhsT_scale=wsc[0][:, a * H + t * P : a * H + (t + 1) * P],
+                    rhs=words[:, cols].bitcast(E4M3),
+                    rhs_scale=plane[:, cells],
+                    start=start and t == 0,
+                    stop=stop and t == PACK - 1,
+                )
+
+        for c in range(CHUNKS):
+            w4_pass(0, c, first[1], slice(c * CELLS, (c + 1) * CELLS), got_sc[1], True, False)
+        for c in range(CHUNKS):
+            w1_pass(0, c, first[0], slice(c * CELLS, (c + 1) * CELLS), False, False)
+        sig = held([P, S * PACK], F32, "sig")
+        for c in range(CHUNKS):
+            h, cc = divmod(c, CHUNKS // 2)
+            cols = slice(cc * CELLS, (cc + 1) * CELLS)
+            w1_pass(1, c, second[0][h], cols, False, False)
+            w4_pass(1, c, second[1][h], cols, soil_sc1, False, True)
+            nc.scalar.activation(
+                sig[:, c * 512 : (c + 1) * 512].rearrange("p (j t) -> p j t", t=PACK),
+                d_banks[c][:].rearrange("p t j -> p j t"),
+                ACT.Sigmoid,
+                scale=-1.0,
+            )
+
+        slope0 = held([P, S], U32, "slope0", "early")
+        gather(slope0[:], tab_w[0][:].bitcast(U32), 2, 0, S)
+        wr_bf = held([P, N * PACK], BF16, "wr_bf")
+        nc.gpsimd.tensor_scalar(
+            wr_bf[:].rearrange("p (s m t) -> p m t s", s=PACK, t=PACK),
+            wr_raw[:].rearrange("p t (m s) -> p m t s", s=PACK),
+            1.0,
+            0.0,
+            ALU.mult,
+            ALU.add,
+        )
+        wr_q = held([P, N], U32, "wr_q")
+        wr_sc = held([P, N], U8, "wr_sc")
+        nc.vector.quantize_mx(wr_q[:].bitcast(E4M3), wr_sc[:], wr_bf[:])
+
+        logs = held([P, S * PACK], F32, "logs", "late")
+        y_q = held([P, S], U32, "y_q")
+        y_sc = held([P, S], U8, "y_sc")
+        y_rows = out_0.rearrange("(p t) j -> p t j", t=PACK)
+        y_words = out_1[0].rearrange("p m t -> p (m t)").bitcast(I32)
+        soft, g_banks, h_bf, y_bf = {}, {}, {}, {}
+
+        def stage_soft(c):
+            span = slice(c * 512, (c + 1) * 512)
+            nc.scalar.activation(logs[:, span], sig[:, span], ACT.Ln, bias=floor[:])
+            soft[c] = ring.tile([P, CELLS, PACK], F32, name="soft")
+            nc.vector.scalar_tensor_tensor(
+                soft[c][:],
+                logs[:, span].rearrange("p (j t) -> p j t", t=PACK),
+                -1.0,
+                d_banks[c][:].rearrange("p t j -> p j t"),
+                ALU.mult,
+                ALU.max,
+            )
+            cells = slice(c * CELLS, (c + 1) * CELLS)
+            g_banks[c] = psum.tile([P, PACK, CELLS], F32, name=f"g{c}", tag=f"bank{c}")
+            for t in range(PACK):
+                for a, words in enumerate((slope0, slope1)):
+                    nc.tensor.matmul_mx(
+                        g_banks[c][:, t, :],
+                        lhsT=w8_q[:, a, t * P : (t + 1) * P].bitcast(E4M3),
+                        lhsT_scale=wsc[1][:, a * H + t * P : a * H + (t + 1) * P],
+                        rhs=words[:, cells].bitcast(E4M3),
+                        rhs_scale=got_sc[2][ROWS * a :, cells],
+                        start=a == 0,
+                        stop=a == PASSES - 1,
+                    )
+
+        def stage_h(c):
+            h_bf[c] = ring.tile([P, CELLS * PACK], BF16, name="h_bf", align_bytes=64)
+            nc.vector.tensor_tensor(
+                h_bf[c][:].rearrange("p (j t) -> p j t", t=PACK),
+                g_banks[c][:].rearrange("p t j -> p j t"),
+                soft[c][:],
+                ALU.mult,
+            )
+
+        def stage_y(c):
+            h_q = ring.tile([P, CELLS], U32, name="h_q", align_bytes=64)
+            h_sc = ring.tile([P, CELLS], U8, name="h_sc", align_bytes=64)
+            nc.vector.quantize_mx(h_q[:].bitcast(E4M3), h_sc[:], h_bf[c][:])
+            bank = psum.tile([P, PACK, CELLS], F32, name=f"y{c}", tag=f"bank{c}")
+            for t in range(PACK):
+                nc.tensor.matmul_mx(
+                    bank[:, t, :],
+                    lhsT=wr_q[:, t * P : (t + 1) * P].bitcast(E4M3),
+                    lhsT_scale=wr_sc[:, t * P : (t + 1) * P],
+                    rhs=h_q[:].bitcast(E4M3),
+                    rhs_scale=h_sc[:],
+                    start=True,
+                    stop=True,
+                )
+            y_bf[c] = ring.tile([P, CELLS * PACK], BF16, name="y_bf", align_bytes=64)
+            nc.scalar.copy(
+                y_bf[c][:].rearrange("p (j t) -> p j t", t=PACK), bank[:].rearrange("p t j -> p j t")
+            )
+            y_sb = ring.tile([P, PACK, CELLS], F32, name="y_sb")
+            nc.scalar.copy(y_sb[:], bank[:])
+            nc.sync.dma_start(y_rows[:, :, c * CELLS : (c + 1) * CELLS], y_sb[:])
+
+        def stage_planes(c):
+            cells = slice(c * CELLS, (c + 1) * CELLS)
+            nc.vector.quantize_mx(y_q[:, cells].bitcast(E4M3), y_sc[:, cells], y_bf[c][:])
+            if c % 2 == 1:
+                pair = slice((c - 1) * CELLS, (c + 1) * CELLS)
+                nc.sync.dma_start(y_words[:, pair], y_q[:, pair].bitcast(I32))
+
+        stages = (stage_soft, stage_h, stage_y, stage_planes)
+        for step in range(CHUNKS + len(stages) - 1):
+            for lag, stage in enumerate(stages):
+                if 0 <= step - lag < CHUNKS:
+                    stage(step - lag)
+        for q in range(QUADS):
+            nc.sync.dma_start(
+                out_2[0, ROWS * q : ROWS * (q + 1), :].bitcast(I32),
+                y_sc[32 * q : 32 * q + ROWS, :].bitcast(I32),
+            )

@@ -25,8 +25,9 @@ ROWS = 4
 CELLS = 128
 CHUNKS = S // CELLS
 HALF = S // 2
-FLOOR = 2.0 ** -60
-LOAD_WORDS = PASSES * (T + H // 2 + PACK * H + H + H // 2) + PACK * N
+LIMIT = 40.0
+SCALAR_ROUNDS = 4
+LOAD_WORDS = T + PASSES * PACK * H
 
 
 def tile_list_runoff_routing_kernel(
@@ -36,7 +37,7 @@ def tile_list_runoff_routing_kernel(
     nc = tc.nc
     with ExitStack() as ctx:
         keep = ctx.enter_context(tc.tile_pool(name="keep", bufs=1))
-        ring = ctx.enter_context(tc.tile_pool(name="ring", bufs=3))
+        ring = ctx.enter_context(tc.tile_pool(name="ring", bufs=4))
         loads = ctx.enter_context(tc.tile_pool(name="loads", bufs=1))
         psum = ctx.enter_context(tc.psum_pool(name="psum", bufs=1))
 
@@ -45,28 +46,31 @@ def tile_list_runoff_routing_kernel(
 
         places = [0]
 
-        def landing(shape, dtype, name):
-            start = places[-1]
-            places.append(start + 4 * math.prod(shape[1:]))
+        def landing(shape, dtype, name, start=None):
+            if start is None:
+                start = places[-1]
+                places.append(start + 4 * math.prod(shape[1:]))
             return loads.tile(shape, dtype, name=name, offset=start)
 
-        tab_sc = held([P, T], U8, "tab_sc")
+        tab_sc = landing([P, T], U8, "tab_sc", 4 * LOAD_WORDS)
         nc.vector.memset(tab_sc[:].bitcast(I32), 0)
         one = loads.tile([P, LOAD_WORDS], F32, name="one", offset=0)
         nc.vector.memset(one[:, 0:1], 1.0)
+        limit = held([P, 1], F32, "limit")
+        nc.vector.tensor_scalar_mul(limit[:], one[:, 0:1], -LIMIT)
         floor = held([P, 1], F32, "floor")
-        nc.vector.tensor_scalar_mul(floor[:], one[:, 0:1], FLOOR)
-        wsc_raw = [landing([P, PASSES * H // 4], I32, f"wsc_raw{k}") for k in range(2)]
+        nc.scalar.activation(floor[:], limit[:], ACT.Sigmoid)
+        wsc_raw = held([P, PASSES * H // 4], I32, "wsc_raw")
         soil_sc1 = held([P, S], U8, "soil_sc1")
-        nc.gpsimd.memset(soil_sc1[:].bitcast(I32), 0)
-        for plane in wsc_raw:
-            nc.gpsimd.memset(plane[:], 0)
-        warm = held([P, 1], F32, "warm")
-        nc.scalar.activation(warm[:], floor[:], ACT.Sigmoid)
+        nc.vector.memset(wsc_raw[:], 0)
+        nc.vector.memset(soil_sc1[:].bitcast(I32), 0)
 
         lists = [held([P, S // 16], U16, f"list{i}") for i in range(3)]
-        for tile, src in zip(lists, (offs, offs2, offs3)):
-            nc.sync.dma_start(tile[:], src)
+        nc.sync.dma_start(lists[1][:], offs2)
+        nc.sync.dma_start(lists[0][:], offs)
+        nc.sync.dma_start(lists[2][:], offs3)
+        w4_raw = held([P, PASSES, H // 2], I32, "w4_raw")
+        nc.sync.dma_start(w4_raw[:], w4_words.bitcast(I32).rearrange("a p c -> p a c"))
         for a in range(PASSES):
             for q in range(QUADS):
                 r0 = 32 * q + ROWS * a
@@ -74,50 +78,43 @@ def tile_list_runoff_routing_kernel(
                     tab_sc[r0 : r0 + ROWS, :].bitcast(I32),
                     tab_scales[a, ROWS * q : ROWS * (q + 1), :].bitcast(I32),
                 )
-        tab_w = [landing([P, T], I32, f"tab_w{a}") for a in range(PASSES)]
+        tab_w = [landing([P, T], I32, "tab_w0"), landing([P, T], I32, "tab_w1", 4 * LOAD_WORDS)]
 
         def load_tab(a):
             nc.sync.dma_start(tab_w[a][:], tab_words[a].rearrange("p n i -> p (n i)").bitcast(I32))
 
-        w4_raw = landing([P, PASSES, H // 2], I32, "w4_raw")
-        nc.sync.dma_start(w4_raw[:], w4_words.bitcast(I32).rearrange("a p c -> p a c"))
-
-        def load_planes(plane, src):
+        def load_planes(src):
             for q in range(QUADS):
                 nc.sync.dma_start(
-                    plane[32 * q : 32 * q + ROWS, :].rearrange("r (a c) -> r a c", a=PASSES),
+                    wsc_raw[32 * q : 32 * q + ROWS, :].rearrange("r (a c) -> r a c", a=PASSES),
                     src[:, ROWS * q : ROWS * (q + 1), :].bitcast(I32).rearrange("a r c -> r a c"),
                 )
 
-        load_planes(wsc_raw[0], w4_scales)
-        load_tab(0)
         w1_raw = [landing([P, PACK, H], F32, f"w1_raw{a}") for a in range(PASSES)]
-        for a in range(PASSES):
+
+        def load_w1(a):
             nc.sync.dma_start(
                 w1_raw[a][:], w1[a * P * PACK : (a + 1) * P * PACK, :].rearrange("(p j) c -> p j c", j=PACK)
             )
-        load_tab(1)
-        w8_raw = landing([P, PASSES, H], I32, "w8_raw")
-        nc.sync.dma_start(
-            w8_raw[:], w8_words.rearrange("a p c i -> a p (c i)").bitcast(I32).rearrange("a p c -> p a c")
-        )
-        wr_raw = landing([P, PACK, N], F32, "wr_raw")
-        wr_rows = wr.rearrange("(q t i) n -> t q i n", t=PACK, i=8)
-        for t in range(PACK):
-            nc.sync.dma_start(wr_raw[:, t, :], wr_rows[t])
-        load_planes(wsc_raw[1], w8_scales)
+
+        load_tab(0)
+        load_planes(w4_scales)
+        load_w1(0)
+        load_w1(1)
 
         def gather(out, window, idx, lo, hi):
             nc.vector.tensor_copy(out, window.indirect(lists[idx][:, lo // 16 : hi // 16]))
 
         got_sc = [held([P, S], U8, f"got_sc{i}") for i in range(3)]
-        for i in (1, 0):
+        for i in (1, 0, 2):
             gather(got_sc[i][:], tab_sc[:], i, 0, S)
         for q in range(QUADS):
-            nc.gpsimd.dma_start(
+            nc.sync.dma_start(
                 soil_sc1[32 * q : 32 * q + ROWS, :].bitcast(I32),
                 got_sc[1][32 * q + ROWS : 32 * q + 2 * ROWS, :].bitcast(I32),
             )
+
+        load_tab(1)
 
         w4_q = held([P, PASSES, H // 2], I32, "w4_q")
         nc.vector.tensor_copy(
@@ -127,12 +124,13 @@ def tile_list_runoff_routing_kernel(
         wsc = [held([P, PASSES * H], U8, f"wsc{k}") for k in range(2)]
 
         def deal_planes(k):
-            nc.vector.tensor_copy(
+            nc.gpsimd.tensor_copy(
                 wsc[k][:].bitcast(I32).rearrange("p (a t q i) -> p a t q i", a=PASSES, t=PACK, i=2),
-                wsc_raw[k][:].rearrange("p (a q t i) -> p a t q i", a=PASSES, t=PACK, i=2),
+                wsc_raw[:].rearrange("p (a q t i) -> p a t q i", a=PASSES, t=PACK, i=2),
             )
 
         deal_planes(0)
+        load_planes(w8_scales)
         first = [held([P, S], U32, f"first{i}") for i in range(2)]
         for i in (1, 0):
             gather(first[i][:], tab_w[0][:].bitcast(U32), i, 0, S)
@@ -145,19 +143,26 @@ def tile_list_runoff_routing_kernel(
             for u in range(2):
                 nc.scalar.copy(dst[:, u], src[:, u])
             nc.vector.quantize_mx(w1_q[a][:].bitcast(E4M3), w1_sc[a][:], grouped[:])
+        w8_raw = landing([P, PASSES, H], I32, "w8_raw", 4 * T)
+        nc.sync.dma_start(
+            w8_raw[:], w8_words.rearrange("a p c i -> a p (c i)").bitcast(I32).rearrange("a p c -> p a c")
+        )
+        wr_raw = landing([P, PACK, N], F32, "wr_raw", 4 * (T + PACK * H))
+        wr_rows = wr.rearrange("(q t i) n -> t q i n", t=PACK, i=8)
+        for t in range(PACK):
+            nc.sync.dma_start(wr_raw[:, t, :], wr_rows[t])
 
-        gather(got_sc[2][:], tab_sc[:], 2, 0, S)
         second = [[None, None] for i in range(2)]
         for h in range(2):
-            for i in range(2):
-                tag = ("early", "late")[h] if i == 1 else None
+            for i in (1, 0):
+                tag = {(1, 0): "early", (0, 1): "late"}.get((i, h))
                 second[i][h] = held([P, HALF], U32, f"second{i}{h}", tag)
                 gather(second[i][h][:], tab_w[1][:].bitcast(U32), i, h * HALF, (h + 1) * HALF)
         slope1 = held([P, S], U32, "slope1")
         gather(slope1[:], tab_w[1][:].bitcast(U32), 2, 0, S)
 
         w8_q = held([P, PASSES, H], I32, "w8_q")
-        nc.vector.tensor_copy(
+        nc.gpsimd.tensor_copy(
             w8_q[:].rearrange("p a (t q i) -> p a t q i", t=PACK, i=8),
             w8_raw[:].rearrange("p a (q t i) -> p a t q i", t=PACK, i=8),
         )
@@ -196,24 +201,26 @@ def tile_list_runoff_routing_kernel(
         for c in range(CHUNKS):
             w1_pass(0, c, first[0], slice(c * CELLS, (c + 1) * CELLS), False, False)
         sig = held([P, S * PACK], F32, "sig")
-        for c in range(CHUNKS):
-            h, cc = divmod(c, CHUNKS // 2)
-            cols = slice(cc * CELLS, (cc + 1) * CELLS)
-            w1_pass(1, c, second[0][h], cols, False, False)
-            w4_pass(1, c, second[1][h], cols, soil_sc1, False, True)
-            nc.scalar.activation(
-                sig[:, c * 512 : (c + 1) * 512].rearrange("p (j t) -> p j t", t=PACK),
-                d_banks[c][:].rearrange("p t j -> p j t"),
-                ACT.Sigmoid,
-                scale=-1.0,
-            )
+        for h in range(2):
+            for cc in range(CHUNKS // 2):
+                cols = slice(cc * CELLS, (cc + 1) * CELLS)
+                w4_pass(1, h * CHUNKS // 2 + cc, second[1][h], cols, soil_sc1, False, False)
+            for cc in range(CHUNKS // 2):
+                c = h * CHUNKS // 2 + cc
+                w1_pass(1, c, second[0][h], slice(cc * CELLS, (cc + 1) * CELLS), False, True)
+                nc.scalar.activation(
+                    sig[:, c * 512 : (c + 1) * 512].rearrange("p (j t) -> p j t", t=PACK),
+                    d_banks[c][:].rearrange("p t j -> p j t"),
+                    ACT.Sigmoid,
+                    scale=-1.0,
+                )
 
         slope0 = held([P, S], U32, "slope0", "early")
         gather(slope0[:], tab_w[0][:].bitcast(U32), 2, 0, S)
         wr_bf = held([P, N * PACK], BF16, "wr_bf")
         nc.gpsimd.tensor_scalar(
-            wr_bf[:].rearrange("p (s m t) -> p m t s", s=PACK, t=PACK),
-            wr_raw[:].rearrange("p t (m s) -> p m t s", s=PACK),
+            wr_bf[:].rearrange("p (s m t) -> p m s t", s=PACK, t=PACK),
+            wr_raw[:].rearrange("p t (m s) -> p m s t", s=PACK),
             1.0,
             0.0,
             ALU.mult,
@@ -281,11 +288,17 @@ def tile_list_runoff_routing_kernel(
                     stop=True,
                 )
             y_bf[c] = ring.tile([P, CELLS * PACK], BF16, name="y_bf", align_bytes=64)
-            nc.scalar.copy(
-                y_bf[c][:].rearrange("p (j t) -> p j t", t=PACK), bank[:].rearrange("p t j -> p j t")
-            )
-            y_sb = ring.tile([P, PACK, CELLS], F32, name="y_sb")
+            y_sb = held([P, PACK, CELLS], F32, f"y_sb{c}")
+            if c < SCALAR_ROUNDS:
+                nc.scalar.copy(
+                    y_bf[c][:].rearrange("p (j t) -> p j t", t=PACK), bank[:].rearrange("p t j -> p j t")
+                )
             nc.scalar.copy(y_sb[:], bank[:])
+            if c >= SCALAR_ROUNDS:
+                nc.vector.tensor_copy(
+                    y_bf[c][:].rearrange("p (j i t) -> p j t i", t=PACK, i=4),
+                    y_sb[:].rearrange("p t (j i) -> p j t i", i=4),
+                )
             nc.sync.dma_start(y_rows[:, :, c * CELLS : (c + 1) * CELLS], y_sb[:])
 
         def stage_planes(c):
@@ -296,8 +309,9 @@ def tile_list_runoff_routing_kernel(
                 nc.sync.dma_start(y_words[:, pair], y_q[:, pair].bitcast(I32))
 
         stages = (stage_soft, stage_h, stage_y, stage_planes)
-        for step in range(CHUNKS + len(stages) - 1):
-            for lag, stage in enumerate(stages):
+        lags = (0, 2, 3, 4)
+        for step in range(CHUNKS + lags[-1]):
+            for lag, stage in zip(lags, stages):
                 if 0 <= step - lag < CHUNKS:
                     stage(step - lag)
         for q in range(QUADS):

@@ -26,8 +26,9 @@ CELLS = 128
 CHUNKS = S // CELLS
 HALF = S // 2
 LIMIT = 40.0
-SCALAR_ROUNDS = 4
-LOAD_WORDS = T + PASSES * PACK * H
+SCALAR_ROUNDS = 5
+PLANE_WORDS = PASSES * 3 * S // 4
+LOAD_WORDS = PACK * H + PLANE_WORDS
 
 
 def tile_list_runoff_routing_kernel(
@@ -53,68 +54,75 @@ def tile_list_runoff_routing_kernel(
             return loads.tile(shape, dtype, name=name, offset=start)
 
         tab_sc = landing([P, T], U8, "tab_sc", 4 * LOAD_WORDS)
-        nc.vector.memset(tab_sc[:].bitcast(I32), 0)
+        nc.vector.memset(tab_sc[32:64, :].bitcast(I32), 0)
+        nc.vector.memset(tab_sc[64:P, :].bitcast(I32), 0)
+        wsc_raw = [held([P, PASSES * H // 4], I32, "wsc_raw0", "first0")]
+        nc.vector.memset(wsc_raw[0][:], 0)
         one = loads.tile([P, LOAD_WORDS], F32, name="one", offset=0)
         nc.vector.memset(one[:, 0:1], 1.0)
         limit = held([P, 1], F32, "limit")
         nc.vector.tensor_scalar_mul(limit[:], one[:, 0:1], -LIMIT)
         floor = held([P, 1], F32, "floor")
         nc.scalar.activation(floor[:], limit[:], ACT.Sigmoid)
-        wsc_raw = held([P, PASSES * H // 4], I32, "wsc_raw")
-        soil_sc1 = held([P, S], U8, "soil_sc1")
-        nc.vector.memset(wsc_raw[:], 0)
-        nc.vector.memset(soil_sc1[:].bitcast(I32), 0)
+        planes = loads.tile([P, PASSES, 3 * S], U8, name="planes", offset=4 * PACK * H, align_bytes=64)
+        nc.gpsimd.memset(planes[:].rearrange("p a s -> p (a s)").bitcast(I32), 0)
 
         lists = [held([P, S // 16], U16, f"list{i}") for i in range(3)]
         nc.sync.dma_start(lists[1][:], offs2)
+        nc.sync.dma_start(tab_sc[0:32, :].bitcast(I32), tab_scales.rearrange("a q t -> (a q) t").bitcast(I32))
         nc.sync.dma_start(lists[0][:], offs)
         nc.sync.dma_start(lists[2][:], offs3)
-        w4_raw = held([P, PASSES, H // 2], I32, "w4_raw")
-        nc.sync.dma_start(w4_raw[:], w4_words.bitcast(I32).rearrange("a p c -> p a c"))
-        for a in range(PASSES):
-            for q in range(QUADS):
-                r0 = 32 * q + ROWS * a
-                nc.sync.dma_start(
-                    tab_sc[r0 : r0 + ROWS, :].bitcast(I32),
-                    tab_scales[a, ROWS * q : ROWS * (q + 1), :].bitcast(I32),
-                )
-        tab_w = [landing([P, T], I32, "tab_w0"), landing([P, T], I32, "tab_w1", 4 * LOAD_WORDS)]
+        tab_w = [held([P, T], I32, "tab_w0"), landing([P, T], I32, "tab_w1", 4 * LOAD_WORDS)]
 
         def load_tab(a):
             nc.sync.dma_start(tab_w[a][:], tab_words[a].rearrange("p n i -> p (n i)").bitcast(I32))
 
-        def load_planes(src):
+        load_tab(0)
+        w4_raw = held([P, PASSES, H // 2], I32, "w4_raw")
+        nc.sync.dma_start(w4_raw[:], w4_words.bitcast(I32).rearrange("a p c -> p a c"))
+
+        def load_planes(k, src):
             for q in range(QUADS):
                 nc.sync.dma_start(
-                    wsc_raw[32 * q : 32 * q + ROWS, :].rearrange("r (a c) -> r a c", a=PASSES),
+                    wsc_raw[k][32 * q : 32 * q + ROWS, :].rearrange("r (a c) -> r a c", a=PASSES),
                     src[:, ROWS * q : ROWS * (q + 1), :].bitcast(I32).rearrange("a r c -> r a c"),
                 )
 
-        w1_raw = [landing([P, PACK, H], F32, f"w1_raw{a}") for a in range(PASSES)]
+        w1_raw = [
+            landing([P, PACK, H], F32, "w1_raw0", 4 * (LOAD_WORDS + T)),
+            landing([P, PACK, H], F32, "w1_raw1", 0),
+        ]
 
         def load_w1(a):
             nc.sync.dma_start(
                 w1_raw[a][:], w1[a * P * PACK : (a + 1) * P * PACK, :].rearrange("(p j) c -> p j c", j=PACK)
             )
 
-        load_tab(0)
-        load_planes(w4_scales)
         load_w1(0)
+        load_planes(0, w4_scales)
         load_w1(1)
 
         def gather(out, window, idx, lo, hi):
             nc.vector.tensor_copy(out, window.indirect(lists[idx][:, lo // 16 : hi // 16]))
 
-        got_sc = [held([P, S], U8, f"got_sc{i}") for i in range(3)]
+        got_sc = held([P, 3 * S], U8, "got_sc")
         for i in (1, 0, 2):
-            gather(got_sc[i][:], tab_sc[:], i, 0, S)
-        for q in range(QUADS):
-            nc.sync.dma_start(
-                soil_sc1[32 * q : 32 * q + ROWS, :].bitcast(I32),
-                got_sc[1][32 * q + ROWS : 32 * q + 2 * ROWS, :].bitcast(I32),
-            )
+            gather(got_sc[:, i * S : (i + 1) * S], tab_sc[:], i, 0, S)
 
+        def move_planes(a):
+            for r in range(ROWS):
+                nc.sync.dma_start(
+                    planes[r:P:32, a, :].bitcast(I32),
+                    got_sc[16 * a + r : 16 * (a + 1) : ROWS, :].bitcast(I32),
+                )
+
+        def plane(i, a, c):
+            return planes[:, a, i * S + c * CELLS : i * S + (c + 1) * CELLS]
+
+        move_planes(0)
         load_tab(1)
+        move_planes(1)
+
 
         w4_q = held([P, PASSES, H // 2], I32, "w4_q")
         nc.vector.tensor_copy(
@@ -124,13 +132,12 @@ def tile_list_runoff_routing_kernel(
         wsc = [held([P, PASSES * H], U8, f"wsc{k}") for k in range(2)]
 
         def deal_planes(k):
-            nc.gpsimd.tensor_copy(
+            nc.vector.tensor_copy(
                 wsc[k][:].bitcast(I32).rearrange("p (a t q i) -> p a t q i", a=PASSES, t=PACK, i=2),
-                wsc_raw[:].rearrange("p (a q t i) -> p a t q i", a=PASSES, t=PACK, i=2),
+                wsc_raw[k][:].rearrange("p (a q t i) -> p a t q i", a=PASSES, t=PACK, i=2),
             )
 
         deal_planes(0)
-        load_planes(w8_scales)
         first = [held([P, S], U32, f"first{i}") for i in range(2)]
         for i in (1, 0):
             gather(first[i][:], tab_w[0][:].bitcast(U32), i, 0, S)
@@ -143,11 +150,14 @@ def tile_list_runoff_routing_kernel(
             for u in range(2):
                 nc.scalar.copy(dst[:, u], src[:, u])
             nc.vector.quantize_mx(w1_q[a][:].bitcast(E4M3), w1_sc[a][:], grouped[:])
-        w8_raw = landing([P, PASSES, H], I32, "w8_raw", 4 * T)
+        w8_raw = landing([P, PASSES, H], I32, "w8_raw", 4 * (LOAD_WORDS + T))
         nc.sync.dma_start(
             w8_raw[:], w8_words.rearrange("a p c i -> a p (c i)").bitcast(I32).rearrange("a p c -> p a c")
         )
-        wr_raw = landing([P, PACK, N], F32, "wr_raw", 4 * (T + PACK * H))
+        wsc_raw.append(landing([P, PASSES * H // 4], I32, "wsc_raw1", 4 * (LOAD_WORDS + T + PASSES * H)))
+        nc.gpsimd.memset(wsc_raw[1][:], 0)
+        load_planes(1, w8_scales)
+        wr_raw = landing([P, PACK, N], F32, "wr_raw", 0)
         wr_rows = wr.rearrange("(q t i) n -> t q i n", t=PACK, i=8)
         for t in range(PACK):
             nc.sync.dma_start(wr_raw[:, t, :], wr_rows[t])
@@ -162,7 +172,7 @@ def tile_list_runoff_routing_kernel(
         gather(slope1[:], tab_w[1][:].bitcast(U32), 2, 0, S)
 
         w8_q = held([P, PASSES, H], I32, "w8_q")
-        nc.gpsimd.tensor_copy(
+        nc.vector.tensor_copy(
             w8_q[:].rearrange("p a (t q i) -> p a t q i", t=PACK, i=8),
             w8_raw[:].rearrange("p a (q t i) -> p a t q i", t=PACK, i=8),
         )
@@ -178,12 +188,12 @@ def tile_list_runoff_routing_kernel(
                     lhsT=w1_q[a][:, t * P : (t + 1) * P].bitcast(E4M3),
                     lhsT_scale=w1_sc[a][:, t * P : (t + 1) * P],
                     rhs=words[:, cols].bitcast(E4M3),
-                    rhs_scale=got_sc[0][ROWS * a :, cells],
+                    rhs_scale=plane(0, a, c),
                     start=start and t == 0,
                     stop=stop and t == PACK - 1,
                 )
 
-        def w4_pass(a, c, words, cols, plane, start, stop):
+        def w4_pass(a, c, words, cols, start, stop):
             cells = slice(c * CELLS, (c + 1) * CELLS)
             for t in range(PACK):
                 nc.tensor.matmul_mx(
@@ -191,20 +201,20 @@ def tile_list_runoff_routing_kernel(
                     lhsT=w4_q[:, a, t * P // 2 : (t + 1) * P // 2].bitcast(U8).bitcast(E2M1),
                     lhsT_scale=wsc[0][:, a * H + t * P : a * H + (t + 1) * P],
                     rhs=words[:, cols].bitcast(E4M3),
-                    rhs_scale=plane[:, cells],
+                    rhs_scale=plane(1, a, c),
                     start=start and t == 0,
                     stop=stop and t == PACK - 1,
                 )
 
         for c in range(CHUNKS):
-            w4_pass(0, c, first[1], slice(c * CELLS, (c + 1) * CELLS), got_sc[1], True, False)
+            w4_pass(0, c, first[1], slice(c * CELLS, (c + 1) * CELLS), True, False)
         for c in range(CHUNKS):
             w1_pass(0, c, first[0], slice(c * CELLS, (c + 1) * CELLS), False, False)
         sig = held([P, S * PACK], F32, "sig")
         for h in range(2):
             for cc in range(CHUNKS // 2):
                 cols = slice(cc * CELLS, (cc + 1) * CELLS)
-                w4_pass(1, h * CHUNKS // 2 + cc, second[1][h], cols, soil_sc1, False, False)
+                w4_pass(1, h * CHUNKS // 2 + cc, second[1][h], cols, False, False)
             for cc in range(CHUNKS // 2):
                 c = h * CHUNKS // 2 + cc
                 w1_pass(1, c, second[0][h], slice(cc * CELLS, (cc + 1) * CELLS), False, True)
@@ -218,14 +228,10 @@ def tile_list_runoff_routing_kernel(
         slope0 = held([P, S], U32, "slope0", "early")
         gather(slope0[:], tab_w[0][:].bitcast(U32), 2, 0, S)
         wr_bf = held([P, N * PACK], BF16, "wr_bf")
-        nc.gpsimd.tensor_scalar(
-            wr_bf[:].rearrange("p (s m t) -> p m s t", s=PACK, t=PACK),
-            wr_raw[:].rearrange("p t (m s) -> p m s t", s=PACK),
-            1.0,
-            0.0,
-            ALU.mult,
-            ALU.add,
-        )
+        wr_dst = wr_bf[:].rearrange("p (s m t) -> p m s t", s=PACK, t=PACK)
+        wr_src = wr_raw[:].rearrange("p t (m s) -> p m s t", s=PACK)
+        nc.scalar.copy(wr_dst[:, : P // 2], wr_src[:, : P // 2])
+        nc.vector.tensor_copy(wr_dst[:, P // 2 :], wr_src[:, P // 2 :])
         wr_q = held([P, N], U32, "wr_q")
         wr_sc = held([P, N], U8, "wr_sc")
         nc.vector.quantize_mx(wr_q[:].bitcast(E4M3), wr_sc[:], wr_bf[:])
@@ -235,12 +241,13 @@ def tile_list_runoff_routing_kernel(
         y_sc = held([P, S], U8, "y_sc")
         y_rows = out_0.rearrange("(p t) j -> p t j", t=PACK)
         y_words = out_1[0].rearrange("p m t -> p (m t)").bitcast(I32)
-        soft, g_banks, h_bf, y_bf = {}, {}, {}, {}
+        y_bf = held([P, S * PACK], BF16, "y_bf")
+        soft, g_banks, h_bf = {}, {}, {}
 
         def stage_soft(c):
             span = slice(c * 512, (c + 1) * 512)
             nc.scalar.activation(logs[:, span], sig[:, span], ACT.Ln, bias=floor[:])
-            soft[c] = ring.tile([P, CELLS, PACK], F32, name="soft")
+            soft[c] = ring.tile([P, CELLS, PACK], F32, name="soft", bufs=3)
             nc.vector.scalar_tensor_tensor(
                 soft[c][:],
                 logs[:, span].rearrange("p (j t) -> p j t", t=PACK),
@@ -258,7 +265,7 @@ def tile_list_runoff_routing_kernel(
                         lhsT=w8_q[:, a, t * P : (t + 1) * P].bitcast(E4M3),
                         lhsT_scale=wsc[1][:, a * H + t * P : a * H + (t + 1) * P],
                         rhs=words[:, cells].bitcast(E4M3),
-                        rhs_scale=got_sc[2][ROWS * a :, cells],
+                        rhs_scale=plane(2, a, c),
                         start=a == 0,
                         stop=a == PASSES - 1,
                     )
@@ -287,25 +294,26 @@ def tile_list_runoff_routing_kernel(
                     start=True,
                     stop=True,
                 )
-            y_bf[c] = ring.tile([P, CELLS * PACK], BF16, name="y_bf", align_bytes=64)
+            rounded = y_bf[:, c * 512 : (c + 1) * 512]
             y_sb = held([P, PACK, CELLS], F32, f"y_sb{c}")
             if c < SCALAR_ROUNDS:
                 nc.scalar.copy(
-                    y_bf[c][:].rearrange("p (j t) -> p j t", t=PACK), bank[:].rearrange("p t j -> p j t")
+                    rounded.rearrange("p (j t) -> p j t", t=PACK), bank[:].rearrange("p t j -> p j t")
                 )
             nc.scalar.copy(y_sb[:], bank[:])
             if c >= SCALAR_ROUNDS:
                 nc.vector.tensor_copy(
-                    y_bf[c][:].rearrange("p (j i t) -> p j t i", t=PACK, i=4),
+                    rounded.rearrange("p (j i t) -> p j t i", t=PACK, i=4),
                     y_sb[:].rearrange("p t (j i) -> p j t i", i=4),
                 )
             nc.sync.dma_start(y_rows[:, :, c * CELLS : (c + 1) * CELLS], y_sb[:])
 
         def stage_planes(c):
-            cells = slice(c * CELLS, (c + 1) * CELLS)
-            nc.vector.quantize_mx(y_q[:, cells].bitcast(E4M3), y_sc[:, cells], y_bf[c][:])
             if c % 2 == 1:
                 pair = slice((c - 1) * CELLS, (c + 1) * CELLS)
+                nc.vector.quantize_mx(
+                    y_q[:, pair].bitcast(E4M3), y_sc[:, pair], y_bf[:, (c - 1) * 512 : (c + 1) * 512]
+                )
                 nc.sync.dma_start(y_words[:, pair], y_q[:, pair].bitcast(I32))
 
         stages = (stage_soft, stage_h, stage_y, stage_planes)

@@ -26,7 +26,7 @@ CELLS = 128
 CHUNKS = S // CELLS
 HALF = S // 2
 LIMIT = 40.0
-SCALAR_ROUNDS = 5
+SCALAR_ROUNDS = 6
 PLANE_WORDS = PASSES * 3 * S // 4
 LOAD_WORDS = PACK * H + PLANE_WORDS
 
@@ -68,8 +68,8 @@ def tile_list_runoff_routing_kernel(
         nc.gpsimd.memset(planes[:].rearrange("p a s -> p (a s)").bitcast(I32), 0)
 
         lists = [held([P, S // 16], U16, f"list{i}") for i in range(3)]
-        nc.sync.dma_start(lists[1][:], offs2)
         nc.sync.dma_start(tab_sc[0:32, :].bitcast(I32), tab_scales.rearrange("a q t -> (a q) t").bitcast(I32))
+        nc.sync.dma_start(lists[1][:], offs2)
         nc.sync.dma_start(lists[0][:], offs)
         nc.sync.dma_start(lists[2][:], offs3)
         tab_w = [held([P, T], I32, "tab_w0"), landing([P, T], I32, "tab_w1", 4 * LOAD_WORDS)]
@@ -210,16 +210,18 @@ def tile_list_runoff_routing_kernel(
             w4_pass(0, c, first[1], slice(c * CELLS, (c + 1) * CELLS), True, False)
         for c in range(CHUNKS):
             w1_pass(0, c, first[0], slice(c * CELLS, (c + 1) * CELLS), False, False)
-        sig = held([P, S * PACK], F32, "sig")
+        sig = [held([P, CELLS * PACK], F32, f"sig{c}") for c in range(CHUNKS)]
         for h in range(2):
-            for cc in range(CHUNKS // 2):
+            for cc in range(CHUNKS // 2 - 1):
                 cols = slice(cc * CELLS, (cc + 1) * CELLS)
                 w4_pass(1, h * CHUNKS // 2 + cc, second[1][h], cols, False, False)
             for cc in range(CHUNKS // 2):
                 c = h * CHUNKS // 2 + cc
+                if cc == CHUNKS // 2 - 1:
+                    w4_pass(1, c, second[1][h], slice(cc * CELLS, (cc + 1) * CELLS), False, False)
                 w1_pass(1, c, second[0][h], slice(cc * CELLS, (cc + 1) * CELLS), False, True)
                 nc.scalar.activation(
-                    sig[:, c * 512 : (c + 1) * 512].rearrange("p (j t) -> p j t", t=PACK),
+                    sig[c][:].rearrange("p (j t) -> p j t", t=PACK),
                     d_banks[c][:].rearrange("p t j -> p j t"),
                     ACT.Sigmoid,
                     scale=-1.0,
@@ -227,14 +229,12 @@ def tile_list_runoff_routing_kernel(
 
         slope0 = held([P, S], U32, "slope0", "early")
         gather(slope0[:], tab_w[0][:].bitcast(U32), 2, 0, S)
-        wr_bf = held([P, N * PACK], BF16, "wr_bf")
+        wr_bf = held([P, N * PACK], BF16, "wr_bf", "tab_w0")
         wr_dst = wr_bf[:].rearrange("p (s m t) -> p m s t", s=PACK, t=PACK)
         wr_src = wr_raw[:].rearrange("p t (m s) -> p m s t", s=PACK)
-        nc.scalar.copy(wr_dst[:, : P // 2], wr_src[:, : P // 2])
-        nc.vector.tensor_copy(wr_dst[:, P // 2 :], wr_src[:, P // 2 :])
-        wr_q = held([P, N], U32, "wr_q")
+        nc.gpsimd.tensor_scalar(wr_dst, wr_src, 1.0, 0.0, ALU.mult, ALU.add)
         wr_sc = held([P, N], U8, "wr_sc")
-        nc.vector.quantize_mx(wr_q[:].bitcast(E4M3), wr_sc[:], wr_bf[:])
+        routing = []
 
         logs = held([P, S * PACK], F32, "logs", "late")
         y_q = held([P, S], U32, "y_q")
@@ -246,7 +246,10 @@ def tile_list_runoff_routing_kernel(
 
         def stage_soft(c):
             span = slice(c * 512, (c + 1) * 512)
-            nc.scalar.activation(logs[:, span], sig[:, span], ACT.Ln, bias=floor[:])
+            nc.scalar.activation(logs[:, span], sig[c][:], ACT.Ln, bias=floor[:])
+            if c == 3:
+                routing.append(held([P, N], U32, "wr_q", "sig3"))
+                nc.vector.quantize_mx(routing[0][:].bitcast(E4M3), wr_sc[:], wr_bf[:])
             soft[c] = ring.tile([P, CELLS, PACK], F32, name="soft", bufs=3)
             nc.vector.scalar_tensor_tensor(
                 soft[c][:],
@@ -287,7 +290,7 @@ def tile_list_runoff_routing_kernel(
             for t in range(PACK):
                 nc.tensor.matmul_mx(
                     bank[:, t, :],
-                    lhsT=wr_q[:, t * P : (t + 1) * P].bitcast(E4M3),
+                    lhsT=routing[0][:, t * P : (t + 1) * P].bitcast(E4M3),
                     lhsT_scale=wr_sc[:, t * P : (t + 1) * P],
                     rhs=h_q[:].bitcast(E4M3),
                     rhs_scale=h_sc[:],

@@ -27,6 +27,7 @@ CHUNKS = S // CELLS
 HALF = S // 2
 LIMIT = 40.0
 SCALAR_ROUNDS = 6
+WR_QUANT_BANK = 4
 PLANE_WORDS = PASSES * 3 * S // 4
 LOAD_WORDS = PACK * H + PLANE_WORDS
 
@@ -64,8 +65,12 @@ def tile_list_runoff_routing_kernel(
         nc.vector.tensor_scalar_mul(limit[:], one[:, 0:1], -LIMIT)
         floor = held([P, 1], F32, "floor")
         nc.scalar.activation(floor[:], limit[:], ACT.Sigmoid)
-        planes = loads.tile([P, PASSES, 3 * S], U8, name="planes", offset=4 * PACK * H, align_bytes=64)
-        nc.gpsimd.memset(planes[:].rearrange("p a s -> p (a s)").bitcast(I32), 0)
+        planes = [
+            loads.tile([P, 3 * S], U8, name=f"planes{a}", offset=4 * PACK * H + a * 3 * S, align_bytes=64)
+            for a in range(PASSES)
+        ]
+        for a in range(PASSES):
+            nc.gpsimd.memset(planes[a][:].bitcast(I32), 0)
 
         lists = [held([P, S // 16], U16, f"list{i}") for i in range(3)]
         nc.sync.dma_start(tab_sc[0:32, :].bitcast(I32), tab_scales.rearrange("a q t -> (a q) t").bitcast(I32))
@@ -112,12 +117,12 @@ def tile_list_runoff_routing_kernel(
         def move_planes(a):
             for r in range(ROWS):
                 nc.sync.dma_start(
-                    planes[r:P:32, a, :].bitcast(I32),
+                    planes[a][r:P:32, :].bitcast(I32),
                     got_sc[16 * a + r : 16 * (a + 1) : ROWS, :].bitcast(I32),
                 )
 
         def plane(i, a, c):
-            return planes[:, a, i * S + c * CELLS : i * S + (c + 1) * CELLS]
+            return planes[a][:, i * S + c * CELLS : i * S + (c + 1) * CELLS]
 
         move_planes(0)
         load_tab(1)
@@ -178,54 +183,43 @@ def tile_list_runoff_routing_kernel(
         )
         deal_planes(1)
 
-        d_banks = [psum.tile([P, PACK, CELLS], F32, name=f"d{c}", tag=f"bank{c}") for c in range(CHUNKS)]
+        d_banks = [psum.tile([P, HALF], F32, name=f"d{b}", tag=f"bank{b}") for b in range(CHUNKS)]
 
-        def w1_pass(a, c, words, cols, start, stop):
-            cells = slice(c * CELLS, (c + 1) * CELLS)
-            for t in range(PACK):
-                nc.tensor.matmul_mx(
-                    d_banks[c][:, t, :],
-                    lhsT=w1_q[a][:, t * P : (t + 1) * P].bitcast(E4M3),
-                    lhsT_scale=w1_sc[a][:, t * P : (t + 1) * P],
-                    rhs=words[:, cols].bitcast(E4M3),
-                    rhs_scale=plane(0, a, c),
-                    start=start and t == 0,
-                    stop=stop and t == PACK - 1,
-                )
+        def w1_pass(a, h, t, words, start, stop):
+            nc.tensor.matmul_mx(
+                d_banks[PACK * h + t][:],
+                lhsT=w1_q[a][:, t * P : (t + 1) * P].bitcast(E4M3),
+                lhsT_scale=w1_sc[a][:, t * P : (t + 1) * P],
+                rhs=words.bitcast(E4M3),
+                rhs_scale=planes[a][:, h * HALF : (h + 1) * HALF],
+                start=start,
+                stop=stop,
+            )
 
-        def w4_pass(a, c, words, cols, start, stop):
-            cells = slice(c * CELLS, (c + 1) * CELLS)
-            for t in range(PACK):
-                nc.tensor.matmul_mx(
-                    d_banks[c][:, t, :],
-                    lhsT=w4_q[:, a, t * P // 2 : (t + 1) * P // 2].bitcast(U8).bitcast(E2M1),
-                    lhsT_scale=wsc[0][:, a * H + t * P : a * H + (t + 1) * P],
-                    rhs=words[:, cols].bitcast(E4M3),
-                    rhs_scale=plane(1, a, c),
-                    start=start and t == 0,
-                    stop=stop and t == PACK - 1,
-                )
+        def w4_pass(a, h, t, words, start, stop):
+            nc.tensor.matmul_mx(
+                d_banks[PACK * h + t][:],
+                lhsT=w4_q[:, a, t * P // 2 : (t + 1) * P // 2].bitcast(U8).bitcast(E2M1),
+                lhsT_scale=wsc[0][:, a * H + t * P : a * H + (t + 1) * P],
+                rhs=words.bitcast(E4M3),
+                rhs_scale=planes[a][:, S + h * HALF : S + (h + 1) * HALF],
+                start=start,
+                stop=stop,
+            )
 
-        for c in range(CHUNKS):
-            w4_pass(0, c, first[1], slice(c * CELLS, (c + 1) * CELLS), True, False)
-        for c in range(CHUNKS):
-            w1_pass(0, c, first[0], slice(c * CELLS, (c + 1) * CELLS), False, False)
-        sig = [held([P, CELLS * PACK], F32, f"sig{c}") for c in range(CHUNKS)]
         for h in range(2):
-            for cc in range(CHUNKS // 2 - 1):
-                cols = slice(cc * CELLS, (cc + 1) * CELLS)
-                w4_pass(1, h * CHUNKS // 2 + cc, second[1][h], cols, False, False)
-            for cc in range(CHUNKS // 2):
-                c = h * CHUNKS // 2 + cc
-                if cc == CHUNKS // 2 - 1:
-                    w4_pass(1, c, second[1][h], slice(cc * CELLS, (cc + 1) * CELLS), False, False)
-                w1_pass(1, c, second[0][h], slice(cc * CELLS, (cc + 1) * CELLS), False, True)
-                nc.scalar.activation(
-                    sig[c][:].rearrange("p (j t) -> p j t", t=PACK),
-                    d_banks[c][:].rearrange("p t j -> p j t"),
-                    ACT.Sigmoid,
-                    scale=-1.0,
-                )
+            for t in range(PACK):
+                w4_pass(0, h, t, first[1][:, h * HALF : (h + 1) * HALF], True, False)
+        for h in range(2):
+            for t in range(PACK):
+                w1_pass(0, h, t, first[0][:, h * HALF : (h + 1) * HALF], False, False)
+        sig = [held([P, HALF], F32, f"sig{b}") for b in range(CHUNKS)]
+        for h in range(2):
+            for t in range(PACK):
+                w4_pass(1, h, t, second[1][h][:], False, False)
+            for t in range(PACK):
+                w1_pass(1, h, t, second[0][h][:], False, True)
+                nc.scalar.activation(sig[PACK * h + t][:], d_banks[PACK * h + t][:], ACT.Sigmoid, scale=-1.0)
 
         slope0 = held([P, S], U32, "slope0", "early")
         gather(slope0[:], tab_w[0][:].bitcast(U32), 2, 0, S)
@@ -242,22 +236,17 @@ def tile_list_runoff_routing_kernel(
         y_rows = out_0.rearrange("(p t) j -> p t j", t=PACK)
         y_words = out_1[0].rearrange("p m t -> p (m t)").bitcast(I32)
         y_bf = held([P, S * PACK], BF16, "y_bf")
-        soft, g_banks, h_bf = {}, {}, {}
+        g_banks, h_bf = {}, {}
+        soft = [held([P, PACK, HALF], F32, f"soft{h}") for h in range(2)]
 
         def stage_soft(c):
             span = slice(c * 512, (c + 1) * 512)
             nc.scalar.activation(logs[:, span], sig[c][:], ACT.Ln, bias=floor[:])
-            if c == 3:
-                routing.append(held([P, N], U32, "wr_q", "sig3"))
+            if c == WR_QUANT_BANK:
+                routing.append(held([P, N], U32, "wr_q", f"sig{WR_QUANT_BANK}"))
                 nc.vector.quantize_mx(routing[0][:].bitcast(E4M3), wr_sc[:], wr_bf[:])
-            soft[c] = ring.tile([P, CELLS, PACK], F32, name="soft", bufs=3)
             nc.vector.scalar_tensor_tensor(
-                soft[c][:],
-                logs[:, span].rearrange("p (j t) -> p j t", t=PACK),
-                -1.0,
-                d_banks[c][:].rearrange("p t j -> p j t"),
-                ALU.mult,
-                ALU.max,
+                soft[c // PACK][:, c % PACK, :], logs[:, span], -1.0, d_banks[c][:], ALU.mult, ALU.max
             )
             cells = slice(c * CELLS, (c + 1) * CELLS)
             g_banks[c] = psum.tile([P, PACK, CELLS], F32, name=f"g{c}", tag=f"bank{c}")
@@ -275,10 +264,11 @@ def tile_list_runoff_routing_kernel(
 
         def stage_h(c):
             h_bf[c] = ring.tile([P, CELLS * PACK], BF16, name="h_bf", align_bytes=64)
+            mine = soft[c // PACK][:, :, c % PACK * CELLS : (c % PACK + 1) * CELLS]
             nc.vector.tensor_tensor(
-                h_bf[c][:].rearrange("p (j t) -> p j t", t=PACK),
-                g_banks[c][:].rearrange("p t j -> p j t"),
-                soft[c][:],
+                h_bf[c][:].rearrange("p (j i t) -> p j t i", t=PACK, i=2),
+                g_banks[c][:].rearrange("p t (j i) -> p j t i", i=2),
+                mine.rearrange("p t (j i) -> p j t i", i=2),
                 ALU.mult,
             )
 
@@ -320,7 +310,7 @@ def tile_list_runoff_routing_kernel(
                 nc.sync.dma_start(y_words[:, pair], y_q[:, pair].bitcast(I32))
 
         stages = (stage_soft, stage_h, stage_y, stage_planes)
-        lags = (0, 2, 3, 4)
+        lags = (0, 3, 4, 5)
         for step in range(CHUNKS + lags[-1]):
             for lag, stage in zip(lags, stages):
                 if 0 <= step - lag < CHUNKS:

@@ -26,10 +26,9 @@ CELLS = 128
 CHUNKS = S // CELLS
 HALF = S // 2
 LIMIT = 40.0
-SCALAR_ROUNDS = 6
-WR_QUANT_BANK = 4
 PLANE_WORDS = PASSES * 3 * S // 4
 LOAD_WORDS = PACK * H + PLANE_WORDS
+SOFT_AT = LOAD_WORDS + T + PACK * H
 
 
 def tile_list_runoff_routing_kernel(
@@ -57,7 +56,7 @@ def tile_list_runoff_routing_kernel(
         tab_sc = landing([P, T], U8, "tab_sc", 4 * LOAD_WORDS)
         nc.vector.memset(tab_sc[32:64, :].bitcast(I32), 0)
         nc.vector.memset(tab_sc[64:P, :].bitcast(I32), 0)
-        wsc_raw = [held([P, PASSES * H // 4], I32, "wsc_raw0", "first0")]
+        wsc_raw = [held([P, PASSES * H // 4], I32, "wsc_raw0")]
         nc.vector.memset(wsc_raw[0][:], 0)
         one = loads.tile([P, LOAD_WORDS], F32, name="one", offset=0)
         nc.vector.memset(one[:, 0:1], 1.0)
@@ -130,14 +129,14 @@ def tile_list_runoff_routing_kernel(
 
 
         w4_q = held([P, PASSES, H // 2], I32, "w4_q")
-        nc.vector.tensor_copy(
+        nc.gpsimd.tensor_copy(
             w4_q[:].rearrange("p a (t q i) -> p a t q i", t=PACK, i=4),
             w4_raw[:].rearrange("p a (q t i) -> p a t q i", t=PACK, i=4),
         )
         wsc = [held([P, PASSES * H], U8, f"wsc{k}") for k in range(2)]
 
         def deal_planes(k):
-            nc.vector.tensor_copy(
+            nc.gpsimd.tensor_copy(
                 wsc[k][:].bitcast(I32).rearrange("p (a t q i) -> p a t q i", a=PASSES, t=PACK, i=2),
                 wsc_raw[k][:].rearrange("p (a q t i) -> p a t q i", a=PASSES, t=PACK, i=2),
             )
@@ -155,6 +154,8 @@ def tile_list_runoff_routing_kernel(
             for u in range(2):
                 nc.scalar.copy(dst[:, u], src[:, u])
             nc.vector.quantize_mx(w1_q[a][:].bitcast(E4M3), w1_sc[a][:], grouped[:])
+        slope0 = [held([P, HALF], U32, "slope00", "w1_bf0")]
+        gather(slope0[0][:], tab_w[0][:].bitcast(U32), 2, 0, HALF)
         w8_raw = landing([P, PASSES, H], I32, "w8_raw", 4 * (LOAD_WORDS + T))
         nc.sync.dma_start(
             w8_raw[:], w8_words.rearrange("a p c i -> a p (c i)").bitcast(I32).rearrange("a p c -> p a c")
@@ -177,7 +178,7 @@ def tile_list_runoff_routing_kernel(
         gather(slope1[:], tab_w[1][:].bitcast(U32), 2, 0, S)
 
         w8_q = held([P, PASSES, H], I32, "w8_q")
-        nc.vector.tensor_copy(
+        nc.gpsimd.tensor_copy(
             w8_q[:].rearrange("p a (t q i) -> p a t q i", t=PACK, i=8),
             w8_raw[:].rearrange("p a (q t i) -> p a t q i", t=PACK, i=8),
         )
@@ -221,14 +222,15 @@ def tile_list_runoff_routing_kernel(
                 w1_pass(1, h, t, second[0][h][:], False, True)
                 nc.scalar.activation(sig[PACK * h + t][:], d_banks[PACK * h + t][:], ACT.Sigmoid, scale=-1.0)
 
-        slope0 = held([P, S], U32, "slope0", "early")
-        gather(slope0[:], tab_w[0][:].bitcast(U32), 2, 0, S)
-        wr_bf = held([P, N * PACK], BF16, "wr_bf", "tab_w0")
+        slope0.append(held([P, HALF], U32, "slope01", "early"))
+        gather(slope0[1][:], tab_w[0][:].bitcast(U32), 2, HALF, S)
+        wr_bf = loads.tile([P, N * PACK], BF16, name="wr_bf", offset=4 * (SOFT_AT + PACK * HALF - N), align_bytes=64)
         wr_dst = wr_bf[:].rearrange("p (s m t) -> p m s t", s=PACK, t=PACK)
         wr_src = wr_raw[:].rearrange("p t (m s) -> p m s t", s=PACK)
         nc.gpsimd.tensor_scalar(wr_dst, wr_src, 1.0, 0.0, ALU.mult, ALU.add)
         wr_sc = held([P, N], U8, "wr_sc")
-        routing = []
+        wr_q = held([P, N], U32, "wr_q")
+        nc.vector.quantize_mx(wr_q[:].bitcast(E4M3), wr_sc[:], wr_bf[:])
 
         logs = held([P, S * PACK], F32, "logs", "late")
         y_q = held([P, S], U32, "y_q")
@@ -237,26 +239,25 @@ def tile_list_runoff_routing_kernel(
         y_words = out_1[0].rearrange("p m t -> p (m t)").bitcast(I32)
         y_bf = held([P, S * PACK], BF16, "y_bf")
         g_banks, h_bf = {}, {}
-        soft = [held([P, PACK, HALF], F32, f"soft{h}") for h in range(2)]
+        for b in range(CHUNKS):
+            nc.scalar.activation(logs[:, b * HALF : (b + 1) * HALF], sig[b][:], ACT.Ln, bias=floor[:])
+        soft = [landing([P, PACK, HALF], F32, f"soft{h}", 4 * (SOFT_AT + h * PACK * HALF)) for h in range(2)]
 
         def stage_soft(c):
             span = slice(c * 512, (c + 1) * 512)
-            nc.scalar.activation(logs[:, span], sig[c][:], ACT.Ln, bias=floor[:])
-            if c == WR_QUANT_BANK:
-                routing.append(held([P, N], U32, "wr_q", f"sig{WR_QUANT_BANK}"))
-                nc.vector.quantize_mx(routing[0][:].bitcast(E4M3), wr_sc[:], wr_bf[:])
             nc.vector.scalar_tensor_tensor(
                 soft[c // PACK][:, c % PACK, :], logs[:, span], -1.0, d_banks[c][:], ALU.mult, ALU.max
             )
             cells = slice(c * CELLS, (c + 1) * CELLS)
+            own = slice(c % PACK * CELLS, (c % PACK + 1) * CELLS)
             g_banks[c] = psum.tile([P, PACK, CELLS], F32, name=f"g{c}", tag=f"bank{c}")
             for t in range(PACK):
-                for a, words in enumerate((slope0, slope1)):
+                for a, words in enumerate((slope0[c // PACK][:, own], slope1[:, cells])):
                     nc.tensor.matmul_mx(
                         g_banks[c][:, t, :],
                         lhsT=w8_q[:, a, t * P : (t + 1) * P].bitcast(E4M3),
                         lhsT_scale=wsc[1][:, a * H + t * P : a * H + (t + 1) * P],
-                        rhs=words[:, cells].bitcast(E4M3),
+                        rhs=words.bitcast(E4M3),
                         rhs_scale=plane(2, a, c),
                         start=a == 0,
                         stop=a == PASSES - 1,
@@ -280,7 +281,7 @@ def tile_list_runoff_routing_kernel(
             for t in range(PACK):
                 nc.tensor.matmul_mx(
                     bank[:, t, :],
-                    lhsT=routing[0][:, t * P : (t + 1) * P].bitcast(E4M3),
+                    lhsT=wr_q[:, t * P : (t + 1) * P].bitcast(E4M3),
                     lhsT_scale=wr_sc[:, t * P : (t + 1) * P],
                     rhs=h_q[:].bitcast(E4M3),
                     rhs_scale=h_sc[:],
@@ -289,32 +290,32 @@ def tile_list_runoff_routing_kernel(
                 )
             rounded = y_bf[:, c * 512 : (c + 1) * 512]
             y_sb = held([P, PACK, CELLS], F32, f"y_sb{c}")
-            if c < SCALAR_ROUNDS:
-                nc.scalar.copy(
-                    rounded.rearrange("p (j t) -> p j t", t=PACK), bank[:].rearrange("p t j -> p j t")
-                )
+            rounder = nc.scalar.copy if c < CHUNKS - 1 else nc.vector.tensor_copy
+            rounder(rounded.rearrange("p (j t) -> p j t", t=PACK), bank[:].rearrange("p t j -> p j t"))
             nc.scalar.copy(y_sb[:], bank[:])
-            if c >= SCALAR_ROUNDS:
-                nc.vector.tensor_copy(
-                    rounded.rearrange("p (j i t) -> p j t i", t=PACK, i=4),
-                    y_sb[:].rearrange("p t (j i) -> p j t i", i=4),
-                )
             nc.sync.dma_start(y_rows[:, :, c * CELLS : (c + 1) * CELLS], y_sb[:])
 
-        def stage_planes(c):
-            if c % 2 == 1:
-                pair = slice((c - 1) * CELLS, (c + 1) * CELLS)
-                nc.vector.quantize_mx(
-                    y_q[:, pair].bitcast(E4M3), y_sc[:, pair], y_bf[:, (c - 1) * 512 : (c + 1) * 512]
-                )
-                nc.sync.dma_start(y_words[:, pair], y_q[:, pair].bitcast(I32))
+        def stage_planes(k):
+            pair = slice(2 * k * CELLS, 2 * (k + 1) * CELLS)
+            nc.vector.quantize_mx(y_q[:, pair].bitcast(E4M3), y_sc[:, pair], y_bf[:, 2 * k * 512 : 2 * (k + 1) * 512])
+            nc.sync.dma_start(y_words[:, pair], y_q[:, pair].bitcast(I32))
 
-        stages = (stage_soft, stage_h, stage_y, stage_planes)
-        lags = (0, 3, 4, 5)
-        for step in range(CHUNKS + lags[-1]):
-            for lag, stage in zip(lags, stages):
-                if 0 <= step - lag < CHUNKS:
-                    stage(step - lag)
+        for c in range(PACK):
+            stage_soft(c)
+        for c in range(PACK):
+            stage_h(c)
+            stage_soft(c + PACK)
+            stage_y(c)
+        for c in range(PACK, CHUNKS - 2):
+            stage_h(c)
+            stage_planes(c - PACK)
+            stage_y(c)
+        stage_h(CHUNKS - 2)
+        stage_h(CHUNKS - 1)
+        stage_y(CHUNKS - 2)
+        stage_planes(2)
+        stage_y(CHUNKS - 1)
+        stage_planes(3)
         for q in range(QUADS):
             nc.sync.dma_start(
                 out_2[0, ROWS * q : ROWS * (q + 1), :].bitcast(I32),

@@ -54,14 +54,12 @@ def tile_list_runoff_routing_kernel(
             return loads.tile(shape, dtype, name=name, offset=start)
 
         tab_sc = landing([P, T], U8, "tab_sc", 4 * LOAD_WORDS)
-        nc.vector.memset(tab_sc[32:64, :].bitcast(I32), 0)
         nc.vector.memset(tab_sc[64:P, :].bitcast(I32), 0)
         wsc_raw = [held([P, PASSES * H // 4], I32, "wsc_raw0")]
-        nc.vector.memset(wsc_raw[0][:], 0)
-        one = loads.tile([P, LOAD_WORDS], F32, name="one", offset=0)
-        nc.vector.memset(one[:, 0:1], 1.0)
+        nc.gpsimd.memset(wsc_raw[0][:], 0)
         limit = held([P, 1], F32, "limit")
-        nc.vector.tensor_scalar_mul(limit[:], one[:, 0:1], -LIMIT)
+        nc.gpsimd.memset(limit[:], -LIMIT)
+        nc.gpsimd.memset(tab_sc[32:64, :].bitcast(I32), 0)
         floor = held([P, 1], F32, "floor")
         nc.scalar.activation(floor[:], limit[:], ACT.Sigmoid)
         planes = [
@@ -154,8 +152,6 @@ def tile_list_runoff_routing_kernel(
             for u in range(2):
                 nc.scalar.copy(dst[:, u], src[:, u])
             nc.vector.quantize_mx(w1_q[a][:].bitcast(E4M3), w1_sc[a][:], grouped[:])
-        slope0 = [held([P, HALF], U32, "slope00", "w1_bf0")]
-        gather(slope0[0][:], tab_w[0][:].bitcast(U32), 2, 0, HALF)
         w8_raw = landing([P, PASSES, H], I32, "w8_raw", 4 * (LOAD_WORDS + T))
         nc.sync.dma_start(
             w8_raw[:], w8_words.rearrange("a p c i -> a p (c i)").bitcast(I32).rearrange("a p c -> p a c")
@@ -222,8 +218,8 @@ def tile_list_runoff_routing_kernel(
                 w1_pass(1, h, t, second[0][h][:], False, True)
                 nc.scalar.activation(sig[PACK * h + t][:], d_banks[PACK * h + t][:], ACT.Sigmoid, scale=-1.0)
 
-        slope0.append(held([P, HALF], U32, "slope01", "early"))
-        gather(slope0[1][:], tab_w[0][:].bitcast(U32), 2, HALF, S)
+        slope0 = held([P, S], U32, "slope0", "early")
+        gather(slope0[:], tab_w[0][:].bitcast(U32), 2, 0, S)
         wr_bf = loads.tile([P, N * PACK], BF16, name="wr_bf", offset=4 * (SOFT_AT + PACK * HALF - N), align_bytes=64)
         wr_dst = wr_bf[:].rearrange("p (s m t) -> p m s t", s=PACK, t=PACK)
         wr_src = wr_raw[:].rearrange("p t (m s) -> p m s t", s=PACK)
@@ -249,10 +245,9 @@ def tile_list_runoff_routing_kernel(
                 soft[c // PACK][:, c % PACK, :], logs[:, span], -1.0, d_banks[c][:], ALU.mult, ALU.max
             )
             cells = slice(c * CELLS, (c + 1) * CELLS)
-            own = slice(c % PACK * CELLS, (c % PACK + 1) * CELLS)
             g_banks[c] = psum.tile([P, PACK, CELLS], F32, name=f"g{c}", tag=f"bank{c}")
             for t in range(PACK):
-                for a, words in enumerate((slope0[c // PACK][:, own], slope1[:, cells])):
+                for a, words in enumerate((slope0[:, cells], slope1[:, cells])):
                     nc.tensor.matmul_mx(
                         g_banks[c][:, t, :],
                         lhsT=w8_q[:, a, t * P : (t + 1) * P].bitcast(E4M3),

@@ -134,7 +134,7 @@ def tile_list_runoff_routing_kernel(
         wsc = [held([P, PASSES * H], U8, f"wsc{k}") for k in range(2)]
 
         def deal_planes(k):
-            nc.gpsimd.tensor_copy(
+            (nc.gpsimd, nc.vector)[k].tensor_copy(
                 wsc[k][:].bitcast(I32).rearrange("p (a t q i) -> p a t q i", a=PASSES, t=PACK, i=2),
                 wsc_raw[k][:].rearrange("p (a q t i) -> p a t q i", a=PASSES, t=PACK, i=2),
             )
@@ -152,17 +152,19 @@ def tile_list_runoff_routing_kernel(
             for u in range(2):
                 nc.scalar.copy(dst[:, u], src[:, u])
             nc.vector.quantize_mx(w1_q[a][:].bitcast(E4M3), w1_sc[a][:], grouped[:])
-        w8_raw = landing([P, PASSES, H], I32, "w8_raw", 4 * (LOAD_WORDS + T))
-        nc.sync.dma_start(
-            w8_raw[:], w8_words.rearrange("a p c i -> a p (c i)").bitcast(I32).rearrange("a p c -> p a c")
-        )
-        wsc_raw.append(landing([P, PASSES * H // 4], I32, "wsc_raw1", 4 * (LOAD_WORDS + T + PASSES * H)))
-        nc.gpsimd.memset(wsc_raw[1][:], 0)
-        load_planes(1, w8_scales)
-        wr_raw = landing([P, PACK, N], F32, "wr_raw", 0)
+        slope0 = [held([P, HALF], U32, "slope00", "w1_bf0")]
+        gather(slope0[0][:], tab_w[0][:].bitcast(U32), 2, 0, HALF)
+        wr_raw = landing([P, PACK, N], F32, "wr_raw", 4 * (LOAD_WORDS + T))
         wr_rows = wr.rearrange("(q t i) n -> t q i n", t=PACK, i=8)
         for t in range(PACK):
             nc.sync.dma_start(wr_raw[:, t, :], wr_rows[t])
+        w8_raw = landing([P, PASSES, H], I32, "w8_raw", 0)
+        nc.sync.dma_start(
+            w8_raw[:], w8_words.rearrange("a p c i -> a p (c i)").bitcast(I32).rearrange("a p c -> p a c")
+        )
+        wsc_raw.append(landing([P, PASSES * H // 4], I32, "wsc_raw1", 4 * PASSES * H))
+        nc.gpsimd.memset(wsc_raw[1][:], 0)
+        load_planes(1, w8_scales)
 
         second = [[None, None] for i in range(2)]
         for h in range(2):
@@ -174,7 +176,7 @@ def tile_list_runoff_routing_kernel(
         gather(slope1[:], tab_w[1][:].bitcast(U32), 2, 0, S)
 
         w8_q = held([P, PASSES, H], I32, "w8_q")
-        nc.gpsimd.tensor_copy(
+        nc.vector.tensor_copy(
             w8_q[:].rearrange("p a (t q i) -> p a t q i", t=PACK, i=8),
             w8_raw[:].rearrange("p a (q t i) -> p a t q i", t=PACK, i=8),
         )
@@ -218,8 +220,8 @@ def tile_list_runoff_routing_kernel(
                 w1_pass(1, h, t, second[0][h][:], False, True)
                 nc.scalar.activation(sig[PACK * h + t][:], d_banks[PACK * h + t][:], ACT.Sigmoid, scale=-1.0)
 
-        slope0 = held([P, S], U32, "slope0", "early")
-        gather(slope0[:], tab_w[0][:].bitcast(U32), 2, 0, S)
+        slope0.append(held([P, HALF], U32, "slope01", "early"))
+        gather(slope0[1][:], tab_w[0][:].bitcast(U32), 2, HALF, S)
         wr_bf = loads.tile([P, N * PACK], BF16, name="wr_bf", offset=4 * (SOFT_AT + PACK * HALF - N), align_bytes=64)
         wr_dst = wr_bf[:].rearrange("p (s m t) -> p m s t", s=PACK, t=PACK)
         wr_src = wr_raw[:].rearrange("p t (m s) -> p m s t", s=PACK)
@@ -245,9 +247,10 @@ def tile_list_runoff_routing_kernel(
                 soft[c // PACK][:, c % PACK, :], logs[:, span], -1.0, d_banks[c][:], ALU.mult, ALU.max
             )
             cells = slice(c * CELLS, (c + 1) * CELLS)
+            own = slice(c % PACK * CELLS, (c % PACK + 1) * CELLS)
             g_banks[c] = psum.tile([P, PACK, CELLS], F32, name=f"g{c}", tag=f"bank{c}")
             for t in range(PACK):
-                for a, words in enumerate((slope0[:, cells], slope1[:, cells])):
+                for a, words in enumerate((slope0[c // PACK][:, own], slope1[:, cells])):
                     nc.tensor.matmul_mx(
                         g_banks[c][:, t, :],
                         lhsT=w8_q[:, a, t * P : (t + 1) * P].bitcast(E4M3),

@@ -26,7 +26,7 @@ CELLS = 128
 CHUNKS = S // CELLS
 HALF = S // 2
 LIMIT = 40.0
-PLANE_WORDS = PASSES * 3 * S // 4
+PLANE_WORDS = PASSES * 2 * S // 4
 LOAD_WORDS = PACK * H + PLANE_WORDS
 SOFT_AT = LOAD_WORDS + T + PACK * H
 
@@ -53,9 +53,9 @@ def tile_list_runoff_routing_kernel(
                 places.append(start + 4 * math.prod(shape[1:]))
             return loads.tile(shape, dtype, name=name, offset=start)
 
-        tab_sc = landing([P, T], U8, "tab_sc", 4 * LOAD_WORDS)
+        tab_sc = held([P, T], U8, "tab_sc")
         nc.vector.memset(tab_sc[64:P, :].bitcast(I32), 0)
-        wsc_raw = [held([P, PASSES * H // 4], I32, "wsc_raw0")]
+        wsc_raw = [landing([P, PASSES * H // 4], I32, "wsc_raw0", 4 * PACK * H + 2 * S)]
         nc.gpsimd.memset(wsc_raw[0][:], 0)
         limit = held([P, 1], F32, "limit")
         nc.gpsimd.memset(limit[:], -LIMIT)
@@ -63,11 +63,10 @@ def tile_list_runoff_routing_kernel(
         floor = held([P, 1], F32, "floor")
         nc.scalar.activation(floor[:], limit[:], ACT.Sigmoid)
         planes = [
-            loads.tile([P, 3 * S], U8, name=f"planes{a}", offset=4 * PACK * H + a * 3 * S, align_bytes=64)
+            loads.tile([P, 2 * S], U8, name=f"planes{a}", offset=4 * PACK * H + a * 2 * S, align_bytes=64)
             for a in range(PASSES)
         ]
-        for a in range(PASSES):
-            nc.gpsimd.memset(planes[a][:].bitcast(I32), 0)
+        nc.gpsimd.memset(planes[0][:].bitcast(I32), 0)
 
         lists = [held([P, S // 16], U16, f"list{i}") for i in range(3)]
         nc.sync.dma_start(tab_sc[0:32, :].bitcast(I32), tab_scales.rearrange("a q t -> (a q) t").bitcast(I32))
@@ -80,7 +79,7 @@ def tile_list_runoff_routing_kernel(
             nc.sync.dma_start(tab_w[a][:], tab_words[a].rearrange("p n i -> p (n i)").bitcast(I32))
 
         load_tab(0)
-        w4_raw = held([P, PASSES, H // 2], I32, "w4_raw")
+        w4_raw = landing([P, PASSES, H // 2], I32, "w4_raw", 4 * LOAD_WORDS)
         nc.sync.dma_start(w4_raw[:], w4_words.bitcast(I32).rearrange("a p c -> p a c"))
 
         def load_planes(k, src):
@@ -107,24 +106,19 @@ def tile_list_runoff_routing_kernel(
         def gather(out, window, idx, lo, hi):
             nc.vector.tensor_copy(out, window.indirect(lists[idx][:, lo // 16 : hi // 16]))
 
-        got_sc = held([P, 3 * S], U8, "got_sc")
-        for i in (1, 0, 2):
+        got_sc = held([P, 2 * S], U8, "got_sc")
+        for i in (1, 0):
             gather(got_sc[:, i * S : (i + 1) * S], tab_sc[:], i, 0, S)
+        got_slope = held([P, S], U8, "got_slope")
+        gather(got_slope[:], tab_sc[:], 2, 0, S)
 
-        def move_planes(a):
+        def move_planes(dst, src, a):
             for r in range(ROWS):
                 nc.sync.dma_start(
-                    planes[a][r:P:32, :].bitcast(I32),
-                    got_sc[16 * a + r : 16 * (a + 1) : ROWS, :].bitcast(I32),
+                    dst[r:P:32, :].bitcast(I32), src[16 * a + r : 16 * (a + 1) : ROWS, :].bitcast(I32)
                 )
 
-        def plane(i, a, c):
-            return planes[a][:, i * S + c * CELLS : i * S + (c + 1) * CELLS]
-
-        move_planes(0)
-        load_tab(1)
-        move_planes(1)
-
+        move_planes(planes[0], got_sc, 0)
 
         w4_q = held([P, PASSES, H // 2], I32, "w4_q")
         nc.gpsimd.tensor_copy(
@@ -139,7 +133,10 @@ def tile_list_runoff_routing_kernel(
                 wsc_raw[k][:].rearrange("p (a q t i) -> p a t q i", a=PASSES, t=PACK, i=2),
             )
 
+        load_tab(1)
         deal_planes(0)
+        nc.gpsimd.memset(planes[1][:].bitcast(I32), 0)
+        move_planes(planes[1], got_sc, 1)
         first = [held([P, S], U32, f"first{i}") for i in range(2)]
         for i in (1, 0):
             gather(first[i][:], tab_w[0][:].bitcast(U32), i, 0, S)
@@ -165,6 +162,12 @@ def tile_list_runoff_routing_kernel(
         wsc_raw.append(landing([P, PASSES * H // 4], I32, "wsc_raw1", 4 * PASSES * H))
         nc.gpsimd.memset(wsc_raw[1][:], 0)
         load_planes(1, w8_scales)
+        slope_planes = []
+        for a in range(PASSES):
+            at = 5 * PASSES * H + a * S
+            slope_planes.append(loads.tile([P, S], U8, name=f"slope_planes{a}", offset=at, align_bytes=64))
+            nc.gpsimd.memset(slope_planes[a][:].bitcast(I32), 0)
+            move_planes(slope_planes[a], got_slope, a)
 
         second = [[None, None] for i in range(2)]
         for h in range(2):
@@ -227,7 +230,7 @@ def tile_list_runoff_routing_kernel(
         wr_src = wr_raw[:].rearrange("p t (m s) -> p m s t", s=PACK)
         nc.gpsimd.tensor_scalar(wr_dst, wr_src, 1.0, 0.0, ALU.mult, ALU.add)
         wr_sc = held([P, N], U8, "wr_sc")
-        wr_q = held([P, N], U32, "wr_q")
+        wr_q = held([P, N], U32, "wr_q", "got_slope")
         nc.vector.quantize_mx(wr_q[:].bitcast(E4M3), wr_sc[:], wr_bf[:])
 
         logs = held([P, S * PACK], F32, "logs", "late")
@@ -256,7 +259,7 @@ def tile_list_runoff_routing_kernel(
                         lhsT=w8_q[:, a, t * P : (t + 1) * P].bitcast(E4M3),
                         lhsT_scale=wsc[1][:, a * H + t * P : a * H + (t + 1) * P],
                         rhs=words.bitcast(E4M3),
-                        rhs_scale=plane(2, a, c),
+                        rhs_scale=slope_planes[a][:, cells],
                         start=a == 0,
                         stop=a == PASSES - 1,
                     )

@@ -1,4 +1,3 @@
-import math
 from contextlib import ExitStack
 
 import concourse.mybir as mybir
@@ -26,9 +25,8 @@ CELLS = 128
 CHUNKS = S // CELLS
 HALF = S // 2
 LIMIT = 40.0
-PLANE_WORDS = PASSES * 2 * S // 4
-LOAD_WORDS = PACK * H + PLANE_WORDS
-SOFT_AT = LOAD_WORDS + T + PACK * H
+RAIN, SOIL, SLOPE = 0, 1, 2
+KIB = 1024
 
 
 def tile_list_runoff_routing_kernel(
@@ -39,78 +37,63 @@ def tile_list_runoff_routing_kernel(
     with ExitStack() as ctx:
         keep = ctx.enter_context(tc.tile_pool(name="keep", bufs=1))
         ring = ctx.enter_context(tc.tile_pool(name="ring", bufs=4))
-        loads = ctx.enter_context(tc.tile_pool(name="loads", bufs=1))
+        shared = ctx.enter_context(tc.tile_pool(name="shared", bufs=1))
         psum = ctx.enter_context(tc.psum_pool(name="psum", bufs=1))
 
         def held(shape, dtype, name, tag=None):
             return keep.tile(shape, dtype, name=name, tag=tag or name, align_bytes=64)
 
-        places = [0]
+        def placed(shape, dtype, name, kib):
+            return shared.tile(shape, dtype, name=name, offset=kib * KIB, align_bytes=64)
 
-        def landing(shape, dtype, name, start=None):
-            if start is None:
-                start = places[-1]
-                places.append(start + 4 * math.prod(shape[1:]))
-            return loads.tile(shape, dtype, name=name, offset=start)
+        def zero(engine, ap):
+            engine.memset(ap.bitcast(I32), 0)
 
         tab_sc = held([P, T], U8, "tab_sc")
-        nc.vector.memset(tab_sc[64:P, :].bitcast(I32), 0)
-        wsc_raw = [landing([P, PASSES * H // 4], I32, "wsc_raw0", 4 * PACK * H + 2 * S)]
-        nc.gpsimd.memset(wsc_raw[0][:], 0)
+        zero(nc.vector, tab_sc[64:P, :])
+        w4_sc_raw = placed([P, PASSES * H], U8, "w4_sc_raw", 10)
+        zero(nc.gpsimd, w4_sc_raw[:])
         limit = held([P, 1], F32, "limit")
         nc.gpsimd.memset(limit[:], -LIMIT)
-        nc.gpsimd.memset(tab_sc[32:64, :].bitcast(I32), 0)
+        zero(nc.gpsimd, tab_sc[32:64, :])
         floor = held([P, 1], F32, "floor")
         nc.scalar.activation(floor[:], limit[:], ACT.Sigmoid)
-        planes = [
-            loads.tile([P, 2 * S], U8, name=f"planes{a}", offset=4 * PACK * H + a * 2 * S, align_bytes=64)
-            for a in range(PASSES)
-        ]
-        nc.gpsimd.memset(planes[0][:].bitcast(I32), 0)
+        d_planes = [placed([P, 2 * S], U8, "d_planes0", 8)]
+        zero(nc.gpsimd, d_planes[0][:])
 
         lists = [held([P, S // 16], U16, f"list{i}") for i in range(3)]
         nc.sync.dma_start(tab_sc[0:32, :].bitcast(I32), tab_scales.rearrange("a q t -> (a q) t").bitcast(I32))
-        nc.sync.dma_start(lists[1][:], offs2)
-        nc.sync.dma_start(lists[0][:], offs)
-        nc.sync.dma_start(lists[2][:], offs3)
-        tab_w = [held([P, T], I32, "tab_w0"), landing([P, T], I32, "tab_w1", 4 * LOAD_WORDS)]
+        nc.sync.dma_start(lists[SOIL][:], offs2)
+        nc.sync.dma_start(lists[RAIN][:], offs)
+        nc.sync.dma_start(lists[SLOPE][:], offs3)
 
-        def load_tab(a):
-            nc.sync.dma_start(tab_w[a][:], tab_words[a].rearrange("p n i -> p (n i)").bitcast(I32))
+        def load_table(tile, a):
+            nc.sync.dma_start(tile[:], tab_words[a].rearrange("p n i -> p (n i)").bitcast(I32))
 
-        load_tab(0)
-        w4_raw = landing([P, PASSES, H // 2], I32, "w4_raw", 4 * LOAD_WORDS)
-        nc.sync.dma_start(w4_raw[:], w4_words.bitcast(I32).rearrange("a p c -> p a c"))
-
-        def load_planes(k, src):
+        def load_scale_rows(tile, src):
             for q in range(QUADS):
                 nc.sync.dma_start(
-                    wsc_raw[k][32 * q : 32 * q + ROWS, :].rearrange("r (a c) -> r a c", a=PASSES),
+                    tile[32 * q : 32 * q + ROWS, :].bitcast(I32).rearrange("r (a c) -> r a c", a=PASSES),
                     src[:, ROWS * q : ROWS * (q + 1), :].bitcast(I32).rearrange("a r c -> r a c"),
                 )
 
-        w1_raw = [
-            landing([P, PACK, H], F32, "w1_raw0", 4 * (LOAD_WORDS + T)),
-            landing([P, PACK, H], F32, "w1_raw1", 0),
-        ]
+        w1_rows = w1.rearrange("(a p j) c -> a p j c", a=PASSES, j=PACK)
+        tab_w = [held([P, T], I32, "tab_w0")]
+        load_table(tab_w[0], 0)
+        w4_raw = placed([P, PASSES, H // 2], I32, "w4_raw", 12)
+        nc.sync.dma_start(w4_raw[:], w4_words.bitcast(I32).rearrange("a p c -> p a c"))
+        load_scale_rows(w4_sc_raw, w4_scales)
+        w1_raw = placed([P, PACK, H], F32, "w1_raw", 0)
+        nc.sync.dma_start(w1_raw[:], w1_rows[0])
 
-        def load_w1(a):
-            nc.sync.dma_start(
-                w1_raw[a][:], w1[a * P * PACK : (a + 1) * P * PACK, :].rearrange("(p j) c -> p j c", j=PACK)
-            )
-
-        load_w1(0)
-        load_planes(0, w4_scales)
-        load_w1(1)
-
-        def gather(out, window, idx, lo, hi):
-            nc.vector.tensor_copy(out, window.indirect(lists[idx][:, lo // 16 : hi // 16]))
+        def gather(out, window, which, lo, hi):
+            nc.vector.tensor_copy(out, window.indirect(lists[which][:, lo // 16 : hi // 16]))
 
         got_sc = held([P, 2 * S], U8, "got_sc")
-        for i in (1, 0):
+        for i in (SOIL, RAIN):
             gather(got_sc[:, i * S : (i + 1) * S], tab_sc[:], i, 0, S)
         got_slope = held([P, S], U8, "got_slope")
-        gather(got_slope[:], tab_sc[:], 2, 0, S)
+        gather(got_slope[:], tab_sc[:], SLOPE, 0, S)
 
         def move_planes(dst, src, a):
             for r in range(ROWS):
@@ -118,153 +101,186 @@ def tile_list_runoff_routing_kernel(
                     dst[r:P:32, :].bitcast(I32), src[16 * a + r : 16 * (a + 1) : ROWS, :].bitcast(I32)
                 )
 
-        move_planes(planes[0], got_sc, 0)
+        move_planes(d_planes[0], got_sc, 0)
 
         w4_q = held([P, PASSES, H // 2], I32, "w4_q")
         nc.gpsimd.tensor_copy(
             w4_q[:].rearrange("p a (t q i) -> p a t q i", t=PACK, i=4),
             w4_raw[:].rearrange("p a (q t i) -> p a t q i", t=PACK, i=4),
         )
-        wsc = [held([P, PASSES * H], U8, f"wsc{k}") for k in range(2)]
+        tab_w.append(placed([P, T], I32, "tab_w1", 12))
+        load_table(tab_w[1], 1)
 
-        def deal_planes(k):
-            (nc.gpsimd, nc.vector)[k].tensor_copy(
-                wsc[k][:].bitcast(I32).rearrange("p (a t q i) -> p a t q i", a=PASSES, t=PACK, i=2),
-                wsc_raw[k][:].rearrange("p (a q t i) -> p a t q i", a=PASSES, t=PACK, i=2),
+        def deal_scales(engine, raw, name):
+            dealt = held([P, PASSES * H], U8, name)
+            engine.tensor_copy(
+                dealt[:].bitcast(I32).rearrange("p (a t q i) -> p a t q i", a=PASSES, t=PACK, i=2),
+                raw[:].bitcast(I32).rearrange("p (a q t i) -> p a t q i", a=PASSES, t=PACK, i=2),
             )
+            return dealt
 
-        load_tab(1)
-        deal_planes(0)
-        nc.gpsimd.memset(planes[1][:].bitcast(I32), 0)
-        move_planes(planes[1], got_sc, 1)
+        w4_sc = deal_scales(nc.gpsimd, w4_sc_raw, "w4_sc")
+        d_planes.append(placed([P, 2 * S], U8, "d_planes1", 10))
+        zero(nc.gpsimd, d_planes[1][:])
+        move_planes(d_planes[1], got_sc, 1)
+
         first = [held([P, S], U32, f"first{i}") for i in range(2)]
-        for i in (1, 0):
+        for i in (SOIL, RAIN):
             gather(first[i][:], tab_w[0][:].bitcast(U32), i, 0, S)
+        w1_bf = [placed([P, H * PACK], BF16, "w1_bf0", 35), placed([P, H * PACK], BF16, "w1_bf1", 56)]
         w1_q = [held([P, H], U32, f"w1_q{a}") for a in range(PASSES)]
         w1_sc = [held([P, H], U8, f"w1_sc{a}") for a in range(PASSES)]
-        for a in range(PASSES):
-            grouped = held([P, H * PACK], BF16, f"w1_bf{a}")
-            dst = grouped[:].rearrange("p (t q u i j) -> p u t q j i", t=PACK, u=2, i=4, j=PACK)
-            src = w1_raw[a][:].rearrange("p j (q t u i) -> p u t q j i", t=PACK, u=2, i=4)
+
+        def round_on_scalar(a, raw, blocks, slices):
+            dst = w1_bf[a][:].rearrange("p (t q u i j) -> p u t q j i", t=PACK, u=2, i=4, j=PACK)
+            src = raw[:].rearrange("p j (q t u i) -> p u t q j i", t=PACK, u=2, i=4)
             for u in range(2):
-                nc.scalar.copy(dst[:, u], src[:, u])
-            nc.vector.quantize_mx(w1_q[a][:].bitcast(E4M3), w1_sc[a][:], grouped[:])
-        slope0 = [held([P, HALF], U32, "slope00", "w1_bf0")]
-        gather(slope0[0][:], tab_w[0][:].bitcast(U32), 2, 0, HALF)
-        wr_raw = landing([P, PACK, N], F32, "wr_raw", 4 * (LOAD_WORDS + T))
+                nc.scalar.copy(dst[:, u, slices, blocks], src[:, u, slices])
+
+        round_on_scalar(0, w1_raw, slice(0, 16), slice(0, PACK))
+        nc.vector.quantize_mx(w1_q[0][:].bitcast(E4M3), w1_sc[0][:], w1_bf[0][:])
+
+        slope0 = [placed([P, HALF], U32, "slope0_a", 36)]
+        gather(slope0[0][:], tab_w[0][:].bitcast(U32), SLOPE, 0, HALF)
+
+        w1_late = [placed([P, PACK, H // 2], F32, f"w1_late{b}", 4 * b) for b in range(2)]
+        for b in range(2):
+            nc.sync.dma_start(w1_late[b][:], w1_rows[1][:, :, b * H // 2 : (b + 1) * H // 2])
+        wr_raw = placed([P, PACK, N], F32, "wr_raw", 28)
         wr_rows = wr.rearrange("(q t i) n -> t q i n", t=PACK, i=8)
         for t in range(PACK):
             nc.sync.dma_start(wr_raw[:, t, :], wr_rows[t])
-        w8_raw = landing([P, PASSES, H], I32, "w8_raw", 0)
+        w8_raw = placed([P, PASSES, H], I32, "w8_raw", 38)
         nc.sync.dma_start(
             w8_raw[:], w8_words.rearrange("a p c i -> a p (c i)").bitcast(I32).rearrange("a p c -> p a c")
         )
-        wsc_raw.append(landing([P, PASSES * H // 4], I32, "wsc_raw1", 4 * PASSES * H))
-        nc.gpsimd.memset(wsc_raw[1][:], 0)
-        load_planes(1, w8_scales)
-        slope_planes = []
-        for a in range(PASSES):
-            at = 5 * PASSES * H + a * S
-            slope_planes.append(loads.tile([P, S], U8, name=f"slope_planes{a}", offset=at, align_bytes=64))
-            nc.gpsimd.memset(slope_planes[a][:].bitcast(I32), 0)
-            move_planes(slope_planes[a], got_slope, a)
 
-        second = [[None, None] for i in range(2)]
-        for h in range(2):
-            for i in (1, 0):
-                tag = {(1, 0): "early", (0, 1): "late"}.get((i, h))
-                second[i][h] = held([P, HALF], U32, f"second{i}{h}", tag)
-                gather(second[i][h][:], tab_w[1][:].bitcast(U32), i, h * HALF, (h + 1) * HALF)
-        slope1 = held([P, S], U32, "slope1")
-        gather(slope1[:], tab_w[1][:].bitcast(U32), 2, 0, S)
-
-        w8_q = held([P, PASSES, H], I32, "w8_q")
-        nc.vector.tensor_copy(
-            w8_q[:].rearrange("p a (t q i) -> p a t q i", t=PACK, i=8),
-            w8_raw[:].rearrange("p a (q t i) -> p a t q i", t=PACK, i=8),
+        second = {
+            (SOIL, 0): held([P, HALF], U32, "soil_a"),
+            (RAIN, 0): held([P, HALF], U32, "rain_a", "rain_then_slope"),
+        }
+        for i, h in second:
+            gather(second[i, h][:], tab_w[1][:].bitcast(U32), i, h * HALF, (h + 1) * HALF)
+        round_on_scalar(1, w1_late[0], slice(0, 8), slice(0, PACK))
+        round_on_scalar(1, w1_late[1], slice(8, 16), slice(0, PACK - 1))
+        nc.gpsimd.tensor_scalar(
+            w1_bf[1][:].rearrange("p (t q i j) -> p t q j i", t=PACK, i=8, j=PACK)[:, PACK - 1, 8:16],
+            w1_late[1][:].rearrange("p j (q t i) -> p t q j i", t=PACK, i=8)[:, PACK - 1],
+            1.0,
+            0.0,
+            ALU.mult,
+            ALU.add,
         )
-        deal_planes(1)
+        nc.vector.quantize_mx(w1_q[1][:].bitcast(E4M3), w1_sc[1][:], w1_bf[1][:])
+        second[SOIL, 1] = placed([P, HALF], U32, "soil_b", 55)
+        second[RAIN, 1] = placed([P, HALF], U32, "rain_b", 57)
+        for i in (SOIL, RAIN):
+            gather(second[i, 1][:], tab_w[1][:].bitcast(U32), i, HALF, S)
+        slope1 = placed([P, S], U32, "slope1", 59)
+        gather(slope1[:], tab_w[1][:].bitcast(U32), SLOPE, 0, S)
+
+        w8_sc_raw = placed([P, PASSES * H], U8, "w8_sc_raw", 0)
+        zero(nc.gpsimd, w8_sc_raw[:])
+        load_scale_rows(w8_sc_raw, w8_scales)
+        g_planes = [placed([P, S], U8, f"g_planes{a}", 1 + a) for a in range(PASSES)]
+        for a in range(PASSES):
+            zero(nc.gpsimd, g_planes[a][:])
+            move_planes(g_planes[a], got_slope, a)
 
         d_banks = [psum.tile([P, HALF], F32, name=f"d{b}", tag=f"bank{b}") for b in range(CHUNKS)]
 
-        def w1_pass(a, h, t, words, start, stop):
+        def w1_pass(a, h, t, words):
             nc.tensor.matmul_mx(
                 d_banks[PACK * h + t][:],
                 lhsT=w1_q[a][:, t * P : (t + 1) * P].bitcast(E4M3),
                 lhsT_scale=w1_sc[a][:, t * P : (t + 1) * P],
                 rhs=words.bitcast(E4M3),
-                rhs_scale=planes[a][:, h * HALF : (h + 1) * HALF],
-                start=start,
-                stop=stop,
+                rhs_scale=d_planes[a][:, RAIN * S + h * HALF : RAIN * S + (h + 1) * HALF],
+                start=False,
+                stop=a == PASSES - 1,
             )
 
-        def w4_pass(a, h, t, words, start, stop):
+        def w4_pass(a, h, t, words):
             nc.tensor.matmul_mx(
                 d_banks[PACK * h + t][:],
                 lhsT=w4_q[:, a, t * P // 2 : (t + 1) * P // 2].bitcast(U8).bitcast(E2M1),
-                lhsT_scale=wsc[0][:, a * H + t * P : a * H + (t + 1) * P],
+                lhsT_scale=w4_sc[:, a * H + t * P : a * H + (t + 1) * P],
                 rhs=words.bitcast(E4M3),
-                rhs_scale=planes[a][:, S + h * HALF : S + (h + 1) * HALF],
-                start=start,
-                stop=stop,
+                rhs_scale=d_planes[a][:, SOIL * S + h * HALF : SOIL * S + (h + 1) * HALF],
+                start=a == 0,
+                stop=False,
             )
 
-        for h in range(2):
-            for t in range(PACK):
-                w4_pass(0, h, t, first[1][:, h * HALF : (h + 1) * HALF], True, False)
-        for h in range(2):
-            for t in range(PACK):
-                w1_pass(0, h, t, first[0][:, h * HALF : (h + 1) * HALF], False, False)
+        for one_pass, i in ((w4_pass, SOIL), (w1_pass, RAIN)):
+            for h in range(2):
+                for t in range(PACK):
+                    one_pass(0, h, t, first[i][:, h * HALF : (h + 1) * HALF])
         sig = [held([P, HALF], F32, f"sig{b}") for b in range(CHUNKS)]
         for h in range(2):
             for t in range(PACK):
-                w4_pass(1, h, t, second[1][h][:], False, False)
+                w4_pass(1, h, t, second[SOIL, h][:])
             for t in range(PACK):
-                w1_pass(1, h, t, second[0][h][:], False, True)
+                w1_pass(1, h, t, second[RAIN, h][:])
                 nc.scalar.activation(sig[PACK * h + t][:], d_banks[PACK * h + t][:], ACT.Sigmoid, scale=-1.0)
 
-        slope0.append(held([P, HALF], U32, "slope01", "early"))
-        gather(slope0[1][:], tab_w[0][:].bitcast(U32), 2, HALF, S)
-        wr_bf = loads.tile([P, N * PACK], BF16, name="wr_bf", offset=4 * (SOFT_AT + PACK * HALF - N), align_bytes=64)
-        wr_dst = wr_bf[:].rearrange("p (s m t) -> p m s t", s=PACK, t=PACK)
-        wr_src = wr_raw[:].rearrange("p t (m s) -> p m s t", s=PACK)
-        nc.gpsimd.tensor_scalar(wr_dst, wr_src, 1.0, 0.0, ALU.mult, ALU.add)
-        wr_sc = held([P, N], U8, "wr_sc")
+        slope0.append(held([P, HALF], U32, "slope0_b", "rain_then_slope"))
+        gather(slope0[1][:], tab_w[0][:].bitcast(U32), SLOPE, HALF, S)
+        w8_q = held([P, PASSES, H], I32, "w8_q")
+        nc.vector.tensor_copy(
+            w8_q[:].rearrange("p a (t q i) -> p a t q i", t=PACK, i=8),
+            w8_raw[:].rearrange("p a (q t i) -> p a t q i", t=PACK, i=8),
+        )
+        w8_sc = deal_scales(nc.vector, w8_sc_raw, "w8_sc")
+
+        wr_bf = placed([P, N * PACK], BF16, "wr_bf", 69)
+        nc.gpsimd.tensor_scalar(
+            wr_bf[:].rearrange("p (s m t) -> p m s t", s=PACK, t=PACK),
+            wr_raw[:].rearrange("p t (m s) -> p m s t", s=PACK),
+            1.0,
+            0.0,
+            ALU.mult,
+            ALU.add,
+        )
         wr_q = held([P, N], U32, "wr_q", "got_slope")
+        wr_sc = held([P, N], U8, "wr_sc")
         nc.vector.quantize_mx(wr_q[:].bitcast(E4M3), wr_sc[:], wr_bf[:])
 
-        logs = held([P, S * PACK], F32, "logs", "late")
-        y_q = held([P, S], U32, "y_q")
-        y_sc = held([P, S], U8, "y_sc")
-        y_rows = out_0.rearrange("(p t) j -> p t j", t=PACK)
-        y_words = out_1[0].rearrange("p m t -> p (m t)").bitcast(I32)
-        y_bf = held([P, S * PACK], BF16, "y_bf")
-        g_banks, h_bf = {}, {}
+        logs = placed([P, S * PACK], F32, "logs", 42)
         for b in range(CHUNKS):
             nc.scalar.activation(logs[:, b * HALF : (b + 1) * HALF], sig[b][:], ACT.Ln, bias=floor[:])
-        soft = [landing([P, PACK, HALF], F32, f"soft{h}", 4 * (SOFT_AT + h * PACK * HALF)) for h in range(2)]
+        soft = [placed([P, PACK, HALF], F32, f"soft{h}", 63 + 8 * h) for h in range(2)]
+        y_q = held([P, S], U32, "y_q")
+        y_sc = held([P, S], U8, "y_sc")
+        y_bf = held([P, S * PACK], BF16, "y_bf")
+        y_rows = out_0.rearrange("(p t) j -> p t j", t=PACK)
+        y_words = out_1[0].rearrange("p m t -> p (m t)").bitcast(I32)
+        g_banks, h_bf, y_banks, y_sb = {}, {}, {}, {}
 
-        def stage_soft(c):
-            span = slice(c * 512, (c + 1) * 512)
+        def softplus_then_g(b):
             nc.vector.scalar_tensor_tensor(
-                soft[c // PACK][:, c % PACK, :], logs[:, span], -1.0, d_banks[c][:], ALU.mult, ALU.max
+                soft[b // PACK][:, b % PACK, :],
+                logs[:, b * HALF : (b + 1) * HALF],
+                -1.0,
+                d_banks[b][:],
+                ALU.mult,
+                ALU.max,
             )
-            cells = slice(c * CELLS, (c + 1) * CELLS)
-            own = slice(c % PACK * CELLS, (c % PACK + 1) * CELLS)
-            g_banks[c] = psum.tile([P, PACK, CELLS], F32, name=f"g{c}", tag=f"bank{c}")
+            cells = slice(b * CELLS, (b + 1) * CELLS)
+            own = slice(b % PACK * CELLS, (b % PACK + 1) * CELLS)
+            g_banks[b] = psum.tile([P, PACK, CELLS], F32, name=f"g{b}", tag=f"bank{b}")
             for t in range(PACK):
-                for a, words in enumerate((slope0[c // PACK][:, own], slope1[:, cells])):
+                for a, words in enumerate((slope0[b // PACK][:, own], slope1[:, cells])):
                     nc.tensor.matmul_mx(
-                        g_banks[c][:, t, :],
+                        g_banks[b][:, t, :],
                         lhsT=w8_q[:, a, t * P : (t + 1) * P].bitcast(E4M3),
-                        lhsT_scale=wsc[1][:, a * H + t * P : a * H + (t + 1) * P],
+                        lhsT_scale=w8_sc[:, a * H + t * P : a * H + (t + 1) * P],
                         rhs=words.bitcast(E4M3),
-                        rhs_scale=slope_planes[a][:, cells],
+                        rhs_scale=g_planes[a][:, cells],
                         start=a == 0,
                         stop=a == PASSES - 1,
                     )
 
-        def stage_h(c):
+        def product(c):
             h_bf[c] = ring.tile([P, CELLS * PACK], BF16, name="h_bf", align_bytes=64)
             mine = soft[c // PACK][:, :, c % PACK * CELLS : (c % PACK + 1) * CELLS]
             nc.vector.tensor_tensor(
@@ -274,49 +290,58 @@ def tile_list_runoff_routing_kernel(
                 ALU.mult,
             )
 
-        def stage_y(c):
+        def route(c):
             h_q = ring.tile([P, CELLS], U32, name="h_q", align_bytes=64)
             h_sc = ring.tile([P, CELLS], U8, name="h_sc", align_bytes=64)
             nc.vector.quantize_mx(h_q[:].bitcast(E4M3), h_sc[:], h_bf[c][:])
-            bank = psum.tile([P, PACK, CELLS], F32, name=f"y{c}", tag=f"bank{c}")
-            for t in range(PACK):
+            y_banks[c] = psum.tile([P, PACK, CELLS], F32, name=f"y{c}", tag=f"bank{c}")
+            for s in range(PACK):
                 nc.tensor.matmul_mx(
-                    bank[:, t, :],
-                    lhsT=wr_q[:, t * P : (t + 1) * P].bitcast(E4M3),
-                    lhsT_scale=wr_sc[:, t * P : (t + 1) * P],
+                    y_banks[c][:, s, :],
+                    lhsT=wr_q[:, s * P : (s + 1) * P].bitcast(E4M3),
+                    lhsT_scale=wr_sc[:, s * P : (s + 1) * P],
                     rhs=h_q[:].bitcast(E4M3),
                     rhs_scale=h_sc[:],
                     start=True,
                     stop=True,
                 )
-            rounded = y_bf[:, c * 512 : (c + 1) * 512]
-            y_sb = held([P, PACK, CELLS], F32, f"y_sb{c}")
-            rounder = nc.scalar.copy if c < CHUNKS - 1 else nc.vector.tensor_copy
-            rounder(rounded.rearrange("p (j t) -> p j t", t=PACK), bank[:].rearrange("p t j -> p j t"))
-            nc.scalar.copy(y_sb[:], bank[:])
-            nc.sync.dma_start(y_rows[:, :, c * CELLS : (c + 1) * CELLS], y_sb[:])
 
-        def stage_planes(k):
+        def round_y(c, copy):
+            rounded = y_bf[:, c * PACK * CELLS : (c + 1) * PACK * CELLS]
+            copy(rounded.rearrange("p (j s) -> p j s", s=PACK), y_banks[c][:].rearrange("p s j -> p j s"))
+
+        def store_y(c):
+            y_sb[c] = held([P, PACK, CELLS], F32, f"y_sb{c}")
+            nc.scalar.copy(y_sb[c][:], y_banks[c][:])
+            nc.sync.dma_start(y_rows[:, :, c * CELLS : (c + 1) * CELLS], y_sb[c][:])
+
+        def store_planes(k):
             pair = slice(2 * k * CELLS, 2 * (k + 1) * CELLS)
-            nc.vector.quantize_mx(y_q[:, pair].bitcast(E4M3), y_sc[:, pair], y_bf[:, 2 * k * 512 : 2 * (k + 1) * 512])
+            wide = slice(2 * k * PACK * CELLS, 2 * (k + 1) * PACK * CELLS)
+            nc.vector.quantize_mx(y_q[:, pair].bitcast(E4M3), y_sc[:, pair], y_bf[:, wide])
             nc.sync.dma_start(y_words[:, pair], y_q[:, pair].bitcast(I32))
 
+        def finish(c):
+            route(c)
+            round_y(c, nc.scalar.copy if c < CHUNKS - 1 else nc.vector.tensor_copy)
+            store_y(c)
+
+        for b in range(PACK):
+            softplus_then_g(b)
         for c in range(PACK):
-            stage_soft(c)
-        for c in range(PACK):
-            stage_h(c)
-            stage_soft(c + PACK)
-            stage_y(c)
+            product(c)
+            softplus_then_g(c + PACK)
+            finish(c)
         for c in range(PACK, CHUNKS - 2):
-            stage_h(c)
-            stage_planes(c - PACK)
-            stage_y(c)
-        stage_h(CHUNKS - 2)
-        stage_h(CHUNKS - 1)
-        stage_y(CHUNKS - 2)
-        stage_planes(2)
-        stage_y(CHUNKS - 1)
-        stage_planes(3)
+            product(c)
+            store_planes(c - PACK)
+            finish(c)
+        product(CHUNKS - 2)
+        product(CHUNKS - 1)
+        finish(CHUNKS - 2)
+        store_planes(2)
+        finish(CHUNKS - 1)
+        store_planes(3)
         for q in range(QUADS):
             nc.sync.dma_start(
                 out_2[0, ROWS * q : ROWS * (q + 1), :].bitcast(I32),

@@ -82,9 +82,10 @@ def tile_list_runoff_routing_kernel(
         load_table(tab_w[0], 0)
         w4_raw = placed([P, PASSES, H // 2], I32, "w4_raw", 12)
         nc.sync.dma_start(w4_raw[:], w4_words.bitcast(I32).rearrange("a p c -> p a c"))
+        w1_raw = [placed([P, PACK, H], F32, "w1_raw0", 28), placed([P, PACK, H], F32, "w1_raw1", 0)]
+        nc.sync.dma_start(w1_raw[0][:], w1_rows[0])
         load_scale_rows(w4_sc_raw, w4_scales)
-        w1_raw = placed([P, PACK, H], F32, "w1_raw", 0)
-        nc.sync.dma_start(w1_raw[:], w1_rows[0])
+        nc.sync.dma_start(w1_raw[1][:], w1_rows[1])
 
         def gather(out, window, which, lo, hi):
             nc.vector.tensor_copy(out, window.indirect(lists[which][:, lo // 16 : hi // 16]))
@@ -127,65 +128,60 @@ def tile_list_runoff_routing_kernel(
         first = [held([P, S], U32, f"first{i}") for i in range(2)]
         for i in (SOIL, RAIN):
             gather(first[i][:], tab_w[0][:].bitcast(U32), i, 0, S)
-        w1_bf = [placed([P, H * PACK], BF16, "w1_bf0", 35), placed([P, H * PACK], BF16, "w1_bf1", 56)]
         w1_q = [held([P, H], U32, f"w1_q{a}") for a in range(PASSES)]
         w1_sc = [held([P, H], U8, f"w1_sc{a}") for a in range(PASSES)]
 
-        def round_on_scalar(a, raw, blocks, slices):
-            dst = w1_bf[a][:].rearrange("p (t q u i j) -> p u t q j i", t=PACK, u=2, i=4, j=PACK)
-            src = raw[:].rearrange("p j (q t u i) -> p u t q j i", t=PACK, u=2, i=4)
+        def quantise_w1(a):
+            w1_bf = held([P, H * PACK], BF16, f"w1_bf{a}")
+            dst = w1_bf[:].rearrange("p (t q u i j) -> p u t q j i", t=PACK, u=2, i=4, j=PACK)
+            src = w1_raw[a][:].rearrange("p j (q t u i) -> p u t q j i", t=PACK, u=2, i=4)
             for u in range(2):
-                nc.scalar.copy(dst[:, u, slices, blocks], src[:, u, slices])
+                nc.scalar.copy(dst[:, u, : PACK - 1], src[:, u, : PACK - 1])
+            nc.gpsimd.tensor_scalar(
+                w1_bf[:].rearrange("p (t q i j) -> p t q j i", t=PACK, i=8, j=PACK)[:, PACK - 1],
+                w1_raw[a][:].rearrange("p j (q t i) -> p t q j i", t=PACK, i=8)[:, PACK - 1],
+                1.0,
+                0.0,
+                ALU.mult,
+                ALU.add,
+            )
+            nc.vector.quantize_mx(w1_q[a][:].bitcast(E4M3), w1_sc[a][:], w1_bf[:])
 
-        round_on_scalar(0, w1_raw, slice(0, 16), slice(0, PACK))
-        nc.vector.quantize_mx(w1_q[0][:].bitcast(E4M3), w1_sc[0][:], w1_bf[0][:])
-
-        slope0 = [placed([P, HALF], U32, "slope0_a", 36)]
+        quantise_w1(0)
+        slope0 = [held([P, HALF], U32, "slope0_a", "w1_bf0")]
         gather(slope0[0][:], tab_w[0][:].bitcast(U32), SLOPE, 0, HALF)
+        quantise_w1(1)
 
-        w1_late = [placed([P, PACK, H // 2], F32, f"w1_late{b}", 4 * b) for b in range(2)]
-        for b in range(2):
-            nc.sync.dma_start(w1_late[b][:], w1_rows[1][:, :, b * H // 2 : (b + 1) * H // 2])
         wr_raw = placed([P, PACK, N], F32, "wr_raw", 28)
         wr_rows = wr.rearrange("(q t i) n -> t q i n", t=PACK, i=8)
         for t in range(PACK):
             nc.sync.dma_start(wr_raw[:, t, :], wr_rows[t])
-        w8_raw = placed([P, PASSES, H], I32, "w8_raw", 38)
+        w8_raw = placed([P, PASSES, H], I32, "w8_raw", 0)
         nc.sync.dma_start(
             w8_raw[:], w8_words.rearrange("a p c i -> a p (c i)").bitcast(I32).rearrange("a p c -> p a c")
         )
-
-        second = {
-            (SOIL, 0): held([P, HALF], U32, "soil_a"),
-            (RAIN, 0): held([P, HALF], U32, "rain_a", "rain_then_slope"),
-        }
-        for i, h in second:
-            gather(second[i, h][:], tab_w[1][:].bitcast(U32), i, h * HALF, (h + 1) * HALF)
-        round_on_scalar(1, w1_late[0], slice(0, 8), slice(0, PACK))
-        round_on_scalar(1, w1_late[1], slice(8, 16), slice(0, PACK - 1))
-        nc.gpsimd.tensor_scalar(
-            w1_bf[1][:].rearrange("p (t q i j) -> p t q j i", t=PACK, i=8, j=PACK)[:, PACK - 1, 8:16],
-            w1_late[1][:].rearrange("p j (q t i) -> p t q j i", t=PACK, i=8)[:, PACK - 1],
-            1.0,
-            0.0,
-            ALU.mult,
-            ALU.add,
-        )
-        nc.vector.quantize_mx(w1_q[1][:].bitcast(E4M3), w1_sc[1][:], w1_bf[1][:])
-        second[SOIL, 1] = placed([P, HALF], U32, "soil_b", 55)
-        second[RAIN, 1] = placed([P, HALF], U32, "rain_b", 57)
-        for i in (SOIL, RAIN):
-            gather(second[i, 1][:], tab_w[1][:].bitcast(U32), i, HALF, S)
-        slope1 = placed([P, S], U32, "slope1", 59)
-        gather(slope1[:], tab_w[1][:].bitcast(U32), SLOPE, 0, S)
-
-        w8_sc_raw = placed([P, PASSES * H], U8, "w8_sc_raw", 0)
+        w8_sc_raw = placed([P, PASSES * H], U8, "w8_sc_raw", 4)
         zero(nc.gpsimd, w8_sc_raw[:])
         load_scale_rows(w8_sc_raw, w8_scales)
-        g_planes = [placed([P, S], U8, f"g_planes{a}", 1 + a) for a in range(PASSES)]
+        g_planes = [placed([P, S], U8, f"g_planes{a}", 5 + a) for a in range(PASSES)]
         for a in range(PASSES):
             zero(nc.gpsimd, g_planes[a][:])
             move_planes(g_planes[a], got_slope, a)
+
+        second = {}
+        for h in range(2):
+            for i in (SOIL, RAIN):
+                tag = {(SOIL, 0): "soil_then_slope", (RAIN, 1): "rain_then_logs"}.get((i, h))
+                second[i, h] = held([P, HALF], U32, f"second{i}{h}", tag)
+                gather(second[i, h][:], tab_w[1][:].bitcast(U32), i, h * HALF, (h + 1) * HALF)
+        slope1 = held([P, S], U32, "slope1")
+        gather(slope1[:], tab_w[1][:].bitcast(U32), SLOPE, 0, S)
+        w8_q = held([P, PASSES, H], I32, "w8_q")
+        nc.vector.tensor_copy(
+            w8_q[:].rearrange("p a (t q i) -> p a t q i", t=PACK, i=8),
+            w8_raw[:].rearrange("p a (q t i) -> p a t q i", t=PACK, i=8),
+        )
+        w8_sc = deal_scales(nc.vector, w8_sc_raw, "w8_sc")
 
         d_banks = [psum.tile([P, HALF], F32, name=f"d{b}", tag=f"bank{b}") for b in range(CHUNKS)]
 
@@ -223,16 +219,10 @@ def tile_list_runoff_routing_kernel(
                 w1_pass(1, h, t, second[RAIN, h][:])
                 nc.scalar.activation(sig[PACK * h + t][:], d_banks[PACK * h + t][:], ACT.Sigmoid, scale=-1.0)
 
-        slope0.append(held([P, HALF], U32, "slope0_b", "rain_then_slope"))
+        slope0.append(held([P, HALF], U32, "slope0_b", "soil_then_slope"))
         gather(slope0[1][:], tab_w[0][:].bitcast(U32), SLOPE, HALF, S)
-        w8_q = held([P, PASSES, H], I32, "w8_q")
-        nc.vector.tensor_copy(
-            w8_q[:].rearrange("p a (t q i) -> p a t q i", t=PACK, i=8),
-            w8_raw[:].rearrange("p a (q t i) -> p a t q i", t=PACK, i=8),
-        )
-        w8_sc = deal_scales(nc.vector, w8_sc_raw, "w8_sc")
 
-        wr_bf = placed([P, N * PACK], BF16, "wr_bf", 69)
+        wr_bf = placed([P, N * PACK], BF16, "wr_bf", 42)
         nc.gpsimd.tensor_scalar(
             wr_bf[:].rearrange("p (s m t) -> p m s t", s=PACK, t=PACK),
             wr_raw[:].rearrange("p t (m s) -> p m s t", s=PACK),
@@ -245,10 +235,10 @@ def tile_list_runoff_routing_kernel(
         wr_sc = held([P, N], U8, "wr_sc")
         nc.vector.quantize_mx(wr_q[:].bitcast(E4M3), wr_sc[:], wr_bf[:])
 
-        logs = placed([P, S * PACK], F32, "logs", 42)
+        logs = held([P, S * PACK], F32, "logs", "rain_then_logs")
         for b in range(CHUNKS):
             nc.scalar.activation(logs[:, b * HALF : (b + 1) * HALF], sig[b][:], ACT.Ln, bias=floor[:])
-        soft = [placed([P, PACK, HALF], F32, f"soft{h}", 63 + 8 * h) for h in range(2)]
+        soft = [placed([P, PACK, HALF], F32, f"soft{h}", 36 + 8 * h) for h in range(2)]
         y_q = held([P, S], U32, "y_q")
         y_sc = held([P, S], U8, "y_sc")
         y_bf = held([P, S * PACK], BF16, "y_bf")
@@ -321,10 +311,20 @@ def tile_list_runoff_routing_kernel(
             nc.vector.quantize_mx(y_q[:, pair].bitcast(E4M3), y_sc[:, pair], y_bf[:, wide])
             nc.sync.dma_start(y_words[:, pair], y_q[:, pair].bitcast(I32))
 
+        def round_stored_y(c):
+            rounded = y_bf[:, c * PACK * CELLS : (c + 1) * PACK * CELLS]
+            nc.vector.tensor_copy(
+                rounded.rearrange("p (j i s) -> p j s i", s=PACK, i=4),
+                y_sb[c][:].rearrange("p s (j i) -> p j s i", i=4),
+            )
+
         def finish(c):
             route(c)
-            round_y(c, nc.scalar.copy if c < CHUNKS - 1 else nc.vector.tensor_copy)
+            if c < PACK:
+                round_y(c, nc.scalar.copy)
             store_y(c)
+            if c >= PACK:
+                round_y(c, nc.scalar.copy)
 
         for b in range(PACK):
             softplus_then_g(b)
@@ -338,9 +338,13 @@ def tile_list_runoff_routing_kernel(
             finish(c)
         product(CHUNKS - 2)
         product(CHUNKS - 1)
-        finish(CHUNKS - 2)
+        route(CHUNKS - 2)
+        store_y(CHUNKS - 2)
+        route(CHUNKS - 1)
         store_planes(2)
-        finish(CHUNKS - 1)
+        round_y(CHUNKS - 1, nc.vector.tensor_copy)
+        store_y(CHUNKS - 1)
+        round_stored_y(CHUNKS - 2)
         store_planes(3)
         for q in range(QUADS):
             nc.sync.dma_start(

@@ -27,6 +27,7 @@ HALF = S // 2
 LIMIT = 40.0
 RAIN, SOIL, SLOPE = 0, 1, 2
 KIB = 1024
+G_BANKS = 3
 
 
 def tile_list_runoff_routing_kernel(
@@ -246,7 +247,7 @@ def tile_list_runoff_routing_kernel(
         y_words = out_1[0].rearrange("p m t -> p (m t)").bitcast(I32)
         g_banks, h_bf, y_banks, y_sb = {}, {}, {}, {}
 
-        def softplus_then_g(b):
+        def softplus(b):
             nc.vector.scalar_tensor_tensor(
                 soft[b // PACK][:, b % PACK, :],
                 logs[:, b * HALF : (b + 1) * HALF],
@@ -255,9 +256,11 @@ def tile_list_runoff_routing_kernel(
                 ALU.mult,
                 ALU.max,
             )
+
+        def project_slope(b):
             cells = slice(b * CELLS, (b + 1) * CELLS)
             own = slice(b % PACK * CELLS, (b % PACK + 1) * CELLS)
-            g_banks[b] = psum.tile([P, PACK, CELLS], F32, name=f"g{b}", tag=f"bank{b}")
+            g_banks[b] = psum.tile([P, PACK, CELLS], F32, name=f"g{b}", tag=f"bank{b % G_BANKS}")
             for t in range(PACK):
                 for a, words in enumerate((slope0[b // PACK][:, own], slope1[:, cells])):
                     nc.tensor.matmul_mx(
@@ -284,7 +287,8 @@ def tile_list_runoff_routing_kernel(
             h_q = ring.tile([P, CELLS], U32, name="h_q", align_bytes=64)
             h_sc = ring.tile([P, CELLS], U8, name="h_sc", align_bytes=64)
             nc.vector.quantize_mx(h_q[:].bitcast(E4M3), h_sc[:], h_bf[c][:])
-            y_banks[c] = psum.tile([P, PACK, CELLS], F32, name=f"y{c}", tag=f"bank{c}")
+            bank = c + G_BANKS if c + G_BANKS < CHUNKS else c % G_BANKS
+            y_banks[c] = psum.tile([P, PACK, CELLS], F32, name=f"y{c}", tag=f"bank{bank}")
             for s in range(PACK):
                 nc.tensor.matmul_mx(
                     y_banks[c][:, s, :],
@@ -327,13 +331,18 @@ def tile_list_runoff_routing_kernel(
                 round_y(c, nc.scalar.copy)
 
         for b in range(PACK):
-            softplus_then_g(b)
+            softplus(b)
+            if b < G_BANKS:
+                project_slope(b)
         for c in range(PACK):
             product(c)
-            softplus_then_g(c + PACK)
+            project_slope(c + G_BANKS)
+            softplus(c + PACK)
             finish(c)
         for c in range(PACK, CHUNKS - 2):
             product(c)
+            if c + G_BANKS < CHUNKS:
+                project_slope(c + G_BANKS)
             store_planes(c - PACK)
             finish(c)
         product(CHUNKS - 2)

@@ -45,21 +45,21 @@ def tile_list_runoff_routing_kernel(
             return keep.tile(shape, dtype, name=name, tag=tag or name, align_bytes=64)
 
         def placed(shape, dtype, name, kib):
-            return shared.tile(shape, dtype, name=name, offset=kib * KIB, align_bytes=64)
+            return shared.tile(shape, dtype, name=name, offset=int(kib * KIB), align_bytes=64)
 
         def zero(engine, ap):
             engine.memset(ap.bitcast(I32), 0)
 
         tab_sc = held([P, T], U8, "tab_sc")
         zero(nc.vector, tab_sc[64:P, :])
-        w4_sc_raw = placed([P, PASSES * H], U8, "w4_sc_raw", 10)
+        zero(nc.vector, tab_sc[32:64, :])
+        w4_sc_raw = placed([P, PASSES * H], U8, "w4_sc_raw", 14)
         zero(nc.gpsimd, w4_sc_raw[:])
         limit = held([P, 1], F32, "limit")
         nc.gpsimd.memset(limit[:], -LIMIT)
-        zero(nc.gpsimd, tab_sc[32:64, :])
         floor = held([P, 1], F32, "floor")
         nc.scalar.activation(floor[:], limit[:], ACT.Sigmoid)
-        d_planes = [placed([P, 2 * S], U8, "d_planes0", 8)]
+        d_planes = [held([P, 2 * S], U8, "early_planes")]
         zero(nc.gpsimd, d_planes[0][:])
 
         lists = [held([P, S // 16], U16, f"list{i}") for i in range(3)]
@@ -81,12 +81,12 @@ def tile_list_runoff_routing_kernel(
         w1_rows = w1.rearrange("(a p j) c -> a p j c", a=PASSES, j=PACK)
         tab_w = [held([P, T], I32, "tab_w0")]
         load_table(tab_w[0], 0)
-        w4_raw = placed([P, PASSES, H // 2], I32, "w4_raw", 12)
+        w4_raw = placed([P, PASSES, H // 2], I32, "w4_raw", 32)
         nc.sync.dma_start(w4_raw[:], w4_words.bitcast(I32).rearrange("a p c -> p a c"))
-        w1_raw = [placed([P, PACK, H], F32, "w1_raw0", 28), placed([P, PACK, H], F32, "w1_raw1", 0)]
-        nc.sync.dma_start(w1_raw[0][:], w1_rows[0])
+        w1_raw = [placed([P, PACK, H], F32, "w1_raw0", 48), placed([P, PACK, H // 2], F32, "w1_raw1", 0)]
         load_scale_rows(w4_sc_raw, w4_scales)
-        nc.sync.dma_start(w1_raw[1][:], w1_rows[1])
+        nc.sync.dma_start(w1_raw[0][:], w1_rows[0])
+        nc.sync.dma_start(w1_raw[1][:], w1_rows[1][:, :, : H // 2])
 
         def gather(out, window, which, lo, hi):
             nc.vector.tensor_copy(out, window.indirect(lists[which][:, lo // 16 : hi // 16]))
@@ -94,13 +94,11 @@ def tile_list_runoff_routing_kernel(
         got_sc = held([P, 2 * S], U8, "got_sc")
         for i in (SOIL, RAIN):
             gather(got_sc[:, i * S : (i + 1) * S], tab_sc[:], i, 0, S)
-        got_slope = held([P, S], U8, "got_slope")
-        gather(got_slope[:], tab_sc[:], SLOPE, 0, S)
 
-        def move_planes(dst, src, a):
+        def move_planes(dst, src, a, row=0):
             for r in range(ROWS):
                 nc.sync.dma_start(
-                    dst[r:P:32, :].bitcast(I32), src[16 * a + r : 16 * (a + 1) : ROWS, :].bitcast(I32)
+                    dst[row + r : P : 32, :].bitcast(I32), src[16 * a + r : 16 * (a + 1) : ROWS, :].bitcast(I32)
                 )
 
         move_planes(d_planes[0], got_sc, 0)
@@ -110,19 +108,21 @@ def tile_list_runoff_routing_kernel(
             w4_q[:].rearrange("p a (t q i) -> p a t q i", t=PACK, i=4),
             w4_raw[:].rearrange("p a (q t i) -> p a t q i", t=PACK, i=4),
         )
-        tab_w.append(placed([P, T], I32, "tab_w1", 12))
+        tab_w.append(placed([P, T], I32, "tab_w1", 32))
         load_table(tab_w[1], 1)
 
         def deal_scales(engine, raw, name):
             dealt = held([P, PASSES * H], U8, name)
             engine.tensor_copy(
                 dealt[:].bitcast(I32).rearrange("p (a t q i) -> p a t q i", a=PASSES, t=PACK, i=2),
-                raw[:].bitcast(I32).rearrange("p (a q t i) -> p a t q i", a=PASSES, t=PACK, i=2),
+                raw.bitcast(I32).rearrange("p (a q t i) -> p a t q i", a=PASSES, t=PACK, i=2),
             )
             return dealt
 
-        w4_sc = deal_scales(nc.gpsimd, w4_sc_raw, "w4_sc")
-        d_planes.append(placed([P, 2 * S], U8, "d_planes1", 10))
+        w4_sc = deal_scales(nc.gpsimd, w4_sc_raw[:], "w4_sc")
+        w1_raw.append(placed([P, PACK, H // 2], F32, "w1_raw2", 10.5))
+        nc.sync.dma_start(w1_raw[2][:], w1_rows[1][:, :, H // 2 :])
+        d_planes.append(placed([P, 2 * S], U8, "d_planes1", 14.5))
         zero(nc.gpsimd, d_planes[1][:])
         move_planes(d_planes[1], got_sc, 1)
 
@@ -132,57 +132,56 @@ def tile_list_runoff_routing_kernel(
         w1_q = [held([P, H], U32, f"w1_q{a}") for a in range(PASSES)]
         w1_sc = [held([P, H], U8, f"w1_sc{a}") for a in range(PASSES)]
 
-        def quantise_w1(a):
-            w1_bf = held([P, H * PACK], BF16, f"w1_bf{a}")
-            dst = w1_bf[:].rearrange("p (t q u i j) -> p u t q j i", t=PACK, u=2, i=4, j=PACK)
-            src = w1_raw[a][:].rearrange("p j (q t u i) -> p u t q j i", t=PACK, u=2, i=4)
+        w1_bf = [held([P, H * PACK], BF16, "w1_bf0"), placed([P, H * PACK], BF16, "w1_bf1", 75.9375)]
+
+        def round_w1(a, raw, blocks):
+            dst = w1_bf[a][:].rearrange("p (t q u i j) -> p u t q j i", t=PACK, u=2, i=4, j=PACK)
+            src = raw[:].rearrange("p j (q t u i) -> p u t q j i", t=PACK, u=2, i=4)
             for u in range(2):
-                nc.scalar.copy(dst[:, u, : PACK - 1], src[:, u, : PACK - 1])
+                nc.scalar.copy(dst[:, u, : PACK - 1, blocks], src[:, u, : PACK - 1])
             nc.gpsimd.tensor_scalar(
-                w1_bf[:].rearrange("p (t q i j) -> p t q j i", t=PACK, i=8, j=PACK)[:, PACK - 1],
-                w1_raw[a][:].rearrange("p j (q t i) -> p t q j i", t=PACK, i=8)[:, PACK - 1],
+                w1_bf[a][:].rearrange("p (t q i j) -> p t q j i", t=PACK, i=8, j=PACK)[:, PACK - 1, blocks],
+                raw[:].rearrange("p j (q t i) -> p t q j i", t=PACK, i=8)[:, PACK - 1],
                 1.0,
                 0.0,
                 ALU.mult,
                 ALU.add,
             )
-            nc.vector.quantize_mx(w1_q[a][:].bitcast(E4M3), w1_sc[a][:], w1_bf[:])
 
+        def quantise_w1(a):
+            nc.vector.quantize_mx(w1_q[a][:].bitcast(E4M3), w1_sc[a][:], w1_bf[a][:])
+
+        round_w1(0, w1_raw[0], slice(0, 16))
         quantise_w1(0)
-        slope0 = [held([P, HALF], U32, "slope0_a", "w1_bf0")]
-        gather(slope0[0][:], tab_w[0][:].bitcast(U32), SLOPE, 0, HALF)
-        quantise_w1(1)
+        got_slope = held([P, S], U8, "got_slope", "w1_bf0")
+        gather(got_slope[:], tab_sc[:], SLOPE, 0, S)
+        round_w1(1, w1_raw[1], slice(0, 8))
+        round_w1(1, w1_raw[2], slice(8, 16))
 
-        wr_raw = placed([P, PACK, N], F32, "wr_raw", 28)
-        wr_rows = wr.rearrange("(q t i) n -> t q i n", t=PACK, i=8)
-        for t in range(PACK):
-            nc.sync.dma_start(wr_raw[:, t, :], wr_rows[t])
-        w8_raw = placed([P, PASSES, H], I32, "w8_raw", 0)
+        w8_raw = placed([P, PASSES, H], I32, "w8_raw", 48)
         nc.sync.dma_start(
             w8_raw[:], w8_words.rearrange("a p c i -> a p (c i)").bitcast(I32).rearrange("a p c -> p a c")
         )
-        w8_sc_raw = placed([P, PASSES * H], U8, "w8_sc_raw", 4)
-        zero(nc.gpsimd, w8_sc_raw[:])
-        load_scale_rows(w8_sc_raw, w8_scales)
-        g_planes = [placed([P, S], U8, f"g_planes{a}", 5 + a) for a in range(PASSES)]
-        for a in range(PASSES):
-            zero(nc.gpsimd, g_planes[a][:])
-            move_planes(g_planes[a], got_slope, a)
+        wr_raw = placed([P, PACK, N], F32, "wr_raw", 0)
+        wr_rows = wr.rearrange("(q t i) n -> t q i n", t=PACK, i=8)
+        for t in range(PACK):
+            nc.sync.dma_start(wr_raw[:, t, :], wr_rows[t])
 
         second = {}
-        for h in range(2):
-            for i in (SOIL, RAIN):
-                tag = {(SOIL, 0): "soil_then_slope", (RAIN, 1): "rain_then_logs"}.get((i, h))
-                second[i, h] = held([P, HALF], U32, f"second{i}{h}", tag)
-                gather(second[i, h][:], tab_w[1][:].bitcast(U32), i, h * HALF, (h + 1) * HALF)
-        slope1 = held([P, S], U32, "slope1")
+        for i in (SOIL, RAIN):
+            second[i, 0] = held([P, HALF], U32, f"second{i}")
+            gather(second[i, 0][:], tab_w[1][:].bitcast(U32), i, 0, HALF)
+        quantise_w1(1)
+        for i, kib in ((SOIL, 76), (RAIN, 74)):
+            second[i, 1] = placed([P, HALF], U32, f"third{i}", kib)
+            gather(second[i, 1][:], tab_w[1][:].bitcast(U32), i, HALF, S)
+        slope1 = placed([P, S], U32, "slope1", 78)
         gather(slope1[:], tab_w[1][:].bitcast(U32), SLOPE, 0, S)
         w8_q = held([P, PASSES, H], I32, "w8_q")
-        nc.vector.tensor_copy(
+        nc.gpsimd.tensor_copy(
             w8_q[:].rearrange("p a (t q i) -> p a t q i", t=PACK, i=8),
             w8_raw[:].rearrange("p a (q t i) -> p a t q i", t=PACK, i=8),
         )
-        w8_sc = deal_scales(nc.vector, w8_sc_raw, "w8_sc")
 
         d_banks = [psum.tile([P, HALF], F32, name=f"d{b}", tag=f"bank{b}") for b in range(CHUNKS)]
 
@@ -212,6 +211,11 @@ def tile_list_runoff_routing_kernel(
             for h in range(2):
                 for t in range(PACK):
                     one_pass(0, h, t, first[i][:, h * HALF : (h + 1) * HALF])
+        w8_sc_raw = d_planes[0][:, : PASSES * H]
+        load_scale_rows(w8_sc_raw, w8_scales)
+        g_planes = d_planes[0][:, S:]
+        for a in range(PASSES):
+            move_planes(g_planes, got_slope, a, ROWS * a)
         sig = [held([P, HALF], F32, f"sig{b}") for b in range(CHUNKS)]
         for h in range(2):
             for t in range(PACK):
@@ -220,10 +224,12 @@ def tile_list_runoff_routing_kernel(
                 w1_pass(1, h, t, second[RAIN, h][:])
                 nc.scalar.activation(sig[PACK * h + t][:], d_banks[PACK * h + t][:], ACT.Sigmoid, scale=-1.0)
 
-        slope0.append(held([P, HALF], U32, "slope0_b", "soil_then_slope"))
-        gather(slope0[1][:], tab_w[0][:].bitcast(U32), SLOPE, HALF, S)
+        slope0 = placed([P, S], U32, "slope0", 72)
+        gather(slope0[:], tab_w[0][:].bitcast(U32), SLOPE, 0, S)
 
-        wr_bf = placed([P, N * PACK], BF16, "wr_bf", 42)
+        w8_sc = deal_scales(nc.vector, w8_sc_raw, "w8_sc")
+
+        wr_bf = placed([P, N * PACK], BF16, "wr_bf", 62)
         nc.gpsimd.tensor_scalar(
             wr_bf[:].rearrange("p (s m t) -> p m s t", s=PACK, t=PACK),
             wr_raw[:].rearrange("p t (m s) -> p m s t", s=PACK),
@@ -232,14 +238,14 @@ def tile_list_runoff_routing_kernel(
             ALU.mult,
             ALU.add,
         )
-        wr_q = held([P, N], U32, "wr_q", "got_slope")
+        wr_q = held([P, N], U32, "wr_q", "w1_bf0")
         wr_sc = held([P, N], U8, "wr_sc")
         nc.vector.quantize_mx(wr_q[:].bitcast(E4M3), wr_sc[:], wr_bf[:])
 
-        logs = held([P, S * PACK], F32, "logs", "rain_then_logs")
+        logs = placed([P, S * PACK], F32, "logs", 16)
         for b in range(CHUNKS):
             nc.scalar.activation(logs[:, b * HALF : (b + 1) * HALF], sig[b][:], ACT.Ln, bias=floor[:])
-        soft = [placed([P, PACK, HALF], F32, f"soft{h}", 36 + 8 * h) for h in range(2)]
+        soft = [placed([P, PACK, HALF], F32, f"soft{h}", 56 + 8 * h) for h in range(2)]
         y_q = held([P, S], U32, "y_q")
         y_sc = held([P, S], U8, "y_sc")
         y_bf = held([P, S * PACK], BF16, "y_bf")
@@ -259,16 +265,15 @@ def tile_list_runoff_routing_kernel(
 
         def project_slope(b):
             cells = slice(b * CELLS, (b + 1) * CELLS)
-            own = slice(b % PACK * CELLS, (b % PACK + 1) * CELLS)
             g_banks[b] = psum.tile([P, PACK, CELLS], F32, name=f"g{b}", tag=f"bank{b % G_BANKS}")
             for t in range(PACK):
-                for a, words in enumerate((slope0[b // PACK][:, own], slope1[:, cells])):
+                for a, words in enumerate((slope0[:, cells], slope1[:, cells])):
                     nc.tensor.matmul_mx(
                         g_banks[b][:, t, :],
                         lhsT=w8_q[:, a, t * P : (t + 1) * P].bitcast(E4M3),
                         lhsT_scale=w8_sc[:, a * H + t * P : a * H + (t + 1) * P],
                         rhs=words.bitcast(E4M3),
-                        rhs_scale=g_planes[a][:, cells],
+                        rhs_scale=g_planes[ROWS * a :, cells],
                         start=a == 0,
                         stop=a == PASSES - 1,
                     )

@@ -19,15 +19,15 @@ ALU = mybir.AluOpType
 P = 128
 PACK = 4
 PASSES = K // (P * PACK)
-QUADS = 4
 ROWS = 4
 CELLS = 128
 CHUNKS = S // CELLS
+QUARTERS = 4
+QUARTER = S // QUARTERS
 HALF = S // 2
 LIMIT = 40.0
-RAIN, SOIL, SLOPE = 0, 1, 2
+SOIL, RAIN, SLOPE = 0, 1, 2
 KIB = 1024
-G_BANKS = 3
 
 
 def tile_list_runoff_routing_kernel(
@@ -41,8 +41,8 @@ def tile_list_runoff_routing_kernel(
         shared = ctx.enter_context(tc.tile_pool(name="shared", bufs=1))
         psum = ctx.enter_context(tc.psum_pool(name="psum", bufs=1))
 
-        def held(shape, dtype, name, tag=None):
-            return keep.tile(shape, dtype, name=name, tag=tag or name, align_bytes=64)
+        def held(shape, dtype, name):
+            return keep.tile(shape, dtype, name=name, tag=name, align_bytes=64)
 
         def placed(shape, dtype, name, kib):
             return shared.tile(shape, dtype, name=name, offset=int(kib * KIB), align_bytes=64)
@@ -53,40 +53,38 @@ def tile_list_runoff_routing_kernel(
         tab_sc = held([P, T], U8, "tab_sc")
         zero(nc.vector, tab_sc[64:P, :])
         zero(nc.vector, tab_sc[32:64, :])
-        w4_sc_raw = placed([P, PASSES * H], U8, "w4_sc_raw", 14)
+        w4_sc_raw = placed([P, PASSES * H], U8, "w4_sc_raw", 16)
         zero(nc.gpsimd, w4_sc_raw[:])
         limit = held([P, 1], F32, "limit")
         nc.gpsimd.memset(limit[:], -LIMIT)
         floor = held([P, 1], F32, "floor")
         nc.scalar.activation(floor[:], limit[:], ACT.Sigmoid)
-        d_planes = [held([P, 2 * S], U8, "early_planes")]
+        d_planes = [held([P, 2 * S], U8, "d_planes0")]
         zero(nc.gpsimd, d_planes[0][:])
 
         lists = [held([P, S // 16], U16, f"list{i}") for i in range(3)]
         nc.sync.dma_start(tab_sc[0:32, :].bitcast(I32), tab_scales.rearrange("a q t -> (a q) t").bitcast(I32))
-        nc.sync.dma_start(lists[SOIL][:], offs2)
-        nc.sync.dma_start(lists[RAIN][:], offs)
-        nc.sync.dma_start(lists[SLOPE][:], offs3)
+        for tile, src in zip(lists, (offs2, offs, offs3)):
+            nc.sync.dma_start(tile[:], src)
 
         def load_table(tile, a):
             nc.sync.dma_start(tile[:], tab_words[a].rearrange("p n i -> p (n i)").bitcast(I32))
 
         def load_scale_rows(tile, src):
-            for q in range(QUADS):
+            for r in range(ROWS):
                 nc.sync.dma_start(
-                    tile[32 * q : 32 * q + ROWS, :].bitcast(I32).rearrange("r (a c) -> r a c", a=PASSES),
-                    src[:, ROWS * q : ROWS * (q + 1), :].bitcast(I32).rearrange("a r c -> r a c"),
+                    tile[r:P:32, :].bitcast(I32).rearrange("q (a c) -> q a c", a=PASSES),
+                    src[:, r:16:ROWS, :].bitcast(I32).rearrange("a q c -> q a c"),
                 )
 
         w1_rows = w1.rearrange("(a p j) c -> a p j c", a=PASSES, j=PACK)
         tab_w = [held([P, T], I32, "tab_w0")]
         load_table(tab_w[0], 0)
-        w4_raw = placed([P, PASSES, H // 2], I32, "w4_raw", 32)
+        w4_raw = placed([P, PASSES, H // 2], I32, "w4_raw", 30)
         nc.sync.dma_start(w4_raw[:], w4_words.bitcast(I32).rearrange("a p c -> p a c"))
-        w1_raw = [placed([P, PACK, H], F32, "w1_raw0", 48), placed([P, PACK, H // 2], F32, "w1_raw1", 0)]
         load_scale_rows(w4_sc_raw, w4_scales)
+        w1_raw = [placed([P, PACK, H], F32, "w1_raw0", 20)]
         nc.sync.dma_start(w1_raw[0][:], w1_rows[0])
-        nc.sync.dma_start(w1_raw[1][:], w1_rows[1][:, :, : H // 2])
 
         def gather(out, window, which, lo, hi):
             nc.vector.tensor_copy(out, window.indirect(lists[which][:, lo // 16 : hi // 16]))
@@ -108,128 +106,130 @@ def tile_list_runoff_routing_kernel(
             w4_q[:].rearrange("p a (t q i) -> p a t q i", t=PACK, i=4),
             w4_raw[:].rearrange("p a (q t i) -> p a t q i", t=PACK, i=4),
         )
-        tab_w.append(placed([P, T], I32, "tab_w1", 32))
-        load_table(tab_w[1], 1)
+        w1_raw.append(placed([P, PACK, H], F32, "w1_raw1", 31))
+        nc.sync.dma_start(w1_raw[1][:], w1_rows[1])
 
-        def deal_scales(engine, raw, name):
-            dealt = held([P, PASSES * H], U8, name)
+        def deal_scales(engine, raw, dealt):
             engine.tensor_copy(
                 dealt[:].bitcast(I32).rearrange("p (a t q i) -> p a t q i", a=PASSES, t=PACK, i=2),
                 raw.bitcast(I32).rearrange("p (a q t i) -> p a t q i", a=PASSES, t=PACK, i=2),
             )
             return dealt
 
-        w4_sc = deal_scales(nc.gpsimd, w4_sc_raw[:], "w4_sc")
-        w1_raw.append(placed([P, PACK, H // 2], F32, "w1_raw2", 10.5))
-        nc.sync.dma_start(w1_raw[2][:], w1_rows[1][:, :, H // 2 :])
-        d_planes.append(placed([P, 2 * S], U8, "d_planes1", 14.5))
+        w4_sc = deal_scales(nc.gpsimd, w4_sc_raw[:], held([P, PASSES * H], U8, "w4_sc"))
+        tab_w.append(placed([P, T], I32, "tab_w1", 0.5))
+        load_table(tab_w[1], 1)
+        d_planes.append(placed([P, 2 * S], U8, "d_planes1", 16.5))
         zero(nc.gpsimd, d_planes[1][:])
         move_planes(d_planes[1], got_sc, 1)
 
-        first = [held([P, S], U32, f"first{i}") for i in range(2)]
+        early = (S, S - QUARTER)
+        first = [held([P, early[i]], U32, f"first{i}") for i in range(2)]
         for i in (SOIL, RAIN):
-            gather(first[i][:], tab_w[0][:].bitcast(U32), i, 0, S)
+            gather(first[i][:], tab_w[0][:].bitcast(U32), i, 0, early[i])
+        got_slope = placed([P, S], U8, "got_slope", 30)
+        gather(got_slope[:], tab_sc[:], SLOPE, 0, S)
         w1_q = [held([P, H], U32, f"w1_q{a}") for a in range(PASSES)]
         w1_sc = [held([P, H], U8, f"w1_sc{a}") for a in range(PASSES)]
 
-        w1_bf = [held([P, H * PACK], BF16, "w1_bf0"), placed([P, H * PACK], BF16, "w1_bf1", 75.9375)]
-
-        def round_w1(a, raw, blocks):
-            dst = w1_bf[a][:].rearrange("p (t q u i j) -> p u t q j i", t=PACK, u=2, i=4, j=PACK)
-            src = raw[:].rearrange("p j (q t u i) -> p u t q j i", t=PACK, u=2, i=4)
+        def quantise_w1(a):
+            w1_bf = placed([P, H * PACK], BF16, f"w1_bf{a}", 76 - 28 * a)
+            dst = w1_bf[:].rearrange("p (t q u i j) -> p u t q j i", t=PACK, u=2, i=4, j=PACK)
+            src = w1_raw[a][:].rearrange("p j (q t u i) -> p u t q j i", t=PACK, u=2, i=4)
             for u in range(2):
-                nc.scalar.copy(dst[:, u, : PACK - 1, blocks], src[:, u, : PACK - 1])
+                nc.scalar.copy(dst[:, u, : PACK - 1], src[:, u, : PACK - 1])
             nc.gpsimd.tensor_scalar(
-                w1_bf[a][:].rearrange("p (t q i j) -> p t q j i", t=PACK, i=8, j=PACK)[:, PACK - 1, blocks],
-                raw[:].rearrange("p j (q t i) -> p t q j i", t=PACK, i=8)[:, PACK - 1],
+                w1_bf[:].rearrange("p (t q i j) -> p t q j i", t=PACK, i=8, j=PACK)[:, PACK - 1],
+                w1_raw[a][:].rearrange("p j (q t i) -> p t q j i", t=PACK, i=8)[:, PACK - 1],
                 1.0,
                 0.0,
                 ALU.mult,
                 ALU.add,
             )
+            nc.vector.quantize_mx(w1_q[a][:].bitcast(E4M3), w1_sc[a][:], w1_bf[:])
 
-        def quantise_w1(a):
-            nc.vector.quantize_mx(w1_q[a][:].bitcast(E4M3), w1_sc[a][:], w1_bf[a][:])
-
-        round_w1(0, w1_raw[0], slice(0, 16))
         quantise_w1(0)
-        got_slope = held([P, S], U8, "got_slope", "w1_bf0")
-        gather(got_slope[:], tab_sc[:], SLOPE, 0, S)
-        round_w1(1, w1_raw[1], slice(0, 8))
-        round_w1(1, w1_raw[2], slice(8, 16))
+        slope = {}
 
-        w8_raw = placed([P, PASSES, H], I32, "w8_raw", 48)
+        def gather_slope(a, h, kib):
+            slope[a, h] = placed([P, HALF], U32, f"slope{a}{h}", kib)
+            gather(slope[a, h][:], tab_w[a][:].bitcast(U32), SLOPE, h * HALF, (h + 1) * HALF)
+
+        gather_slope(0, 0, 25)
+        quantise_w1(1)
+        first_tail = placed([P, QUARTER], U32, "first_tail", 50.5)
+        gather(first_tail[:], tab_w[0][:].bitcast(U32), RAIN, early[RAIN], S)
+
+        w8_raw = placed([P, PASSES, H], I32, "w8_raw", 20)
         nc.sync.dma_start(
             w8_raw[:], w8_words.rearrange("a p c i -> a p (c i)").bitcast(I32).rearrange("a p c -> p a c")
         )
-        wr_raw = placed([P, PACK, N], F32, "wr_raw", 0)
+        w8_sc_raw = placed([P, PASSES * H], U8, "w8_sc_raw", 24)
+        zero(nc.gpsimd, w8_sc_raw[:])
+        load_scale_rows(w8_sc_raw, w8_scales)
+        wr_raw = placed([P, PACK, N], F32, "wr_raw", 38.5)
         wr_rows = wr.rearrange("(q t i) n -> t q i n", t=PACK, i=8)
         for t in range(PACK):
             nc.sync.dma_start(wr_raw[:, t, :], wr_rows[t])
 
         second = {}
-        for i in (SOIL, RAIN):
-            second[i, 0] = held([P, HALF], U32, f"second{i}")
-            gather(second[i, 0][:], tab_w[1][:].bitcast(U32), i, 0, HALF)
-        quantise_w1(1)
-        for i, kib in ((SOIL, 76), (RAIN, 74)):
-            second[i, 1] = placed([P, HALF], U32, f"third{i}", kib)
-            gather(second[i, 1][:], tab_w[1][:].bitcast(U32), i, HALF, S)
-        slope1 = placed([P, S], U32, "slope1", 78)
-        gather(slope1[:], tab_w[1][:].bitcast(U32), SLOPE, 0, S)
+        for c in range(QUARTERS):
+            for i in (SOIL, RAIN):
+                second[i, c] = placed([P, QUARTER], U32, f"second{i}{c}", (32 if c < 3 else 42.5) + 2 * c + i)
+                gather(second[i, c][:], tab_w[1][:].bitcast(U32), i, c * QUARTER, (c + 1) * QUARTER)
+        gather_slope(1, 0, 51.5)
         w8_q = held([P, PASSES, H], I32, "w8_q")
         nc.gpsimd.tensor_copy(
             w8_q[:].rearrange("p a (t q i) -> p a t q i", t=PACK, i=8),
             w8_raw[:].rearrange("p a (q t i) -> p a t q i", t=PACK, i=8),
         )
+        w8_sc = deal_scales(nc.gpsimd, w8_sc_raw[:], held([P, PASSES * H], U8, "w8_sc"))
 
-        d_banks = [psum.tile([P, HALF], F32, name=f"d{b}", tag=f"bank{b}") for b in range(CHUNKS)]
+        d_banks = [psum.tile([P, 2, QUARTER], F32, name=f"d{b}", tag=f"bank{b}") for b in range(CHUNKS)]
 
-        def w1_pass(a, h, t, words):
+        def d_pass(i, a, c, t):
+            cells = slice(c * QUARTER, (c + 1) * QUARTER)
+            if a == 1:
+                words = second[i, c][:]
+            else:
+                words = first[i][:, cells] if cells.stop <= early[i] else first_tail[:]
+            if i == SOIL:
+                lhsT = w4_q[:, a, t * P // 2 : (t + 1) * P // 2].bitcast(U8).bitcast(E2M1)
+                lhsT_scale = w4_sc[:, a * H + t * P : a * H + (t + 1) * P]
+            else:
+                lhsT = w1_q[a][:, t * P : (t + 1) * P].bitcast(E4M3)
+                lhsT_scale = w1_sc[a][:, t * P : (t + 1) * P]
             nc.tensor.matmul_mx(
-                d_banks[PACK * h + t][:],
-                lhsT=w1_q[a][:, t * P : (t + 1) * P].bitcast(E4M3),
-                lhsT_scale=w1_sc[a][:, t * P : (t + 1) * P],
+                d_banks[2 * c + t // 2][:, t % 2, :],
+                lhsT=lhsT,
+                lhsT_scale=lhsT_scale,
                 rhs=words.bitcast(E4M3),
-                rhs_scale=d_planes[a][:, RAIN * S + h * HALF : RAIN * S + (h + 1) * HALF],
-                start=False,
-                stop=a == PASSES - 1,
+                rhs_scale=d_planes[a][:, i * S + c * QUARTER : i * S + (c + 1) * QUARTER],
+                start=(i, a, t % 2) == (SOIL, 0, 0),
+                stop=(i, a, t % 2) == (RAIN, PASSES - 1, 1),
             )
 
-        def w4_pass(a, h, t, words):
-            nc.tensor.matmul_mx(
-                d_banks[PACK * h + t][:],
-                lhsT=w4_q[:, a, t * P // 2 : (t + 1) * P // 2].bitcast(U8).bitcast(E2M1),
-                lhsT_scale=w4_sc[:, a * H + t * P : a * H + (t + 1) * P],
-                rhs=words.bitcast(E4M3),
-                rhs_scale=d_planes[a][:, SOIL * S + h * HALF : SOIL * S + (h + 1) * HALF],
-                start=a == 0,
-                stop=False,
-            )
-
-        for one_pass, i in ((w4_pass, SOIL), (w1_pass, RAIN)):
-            for h in range(2):
+        for i in (SOIL, RAIN):
+            for c in range(QUARTERS):
                 for t in range(PACK):
-                    one_pass(0, h, t, first[i][:, h * HALF : (h + 1) * HALF])
-        w8_sc_raw = d_planes[0][:, : PASSES * H]
-        load_scale_rows(w8_sc_raw, w8_scales)
-        g_planes = d_planes[0][:, S:]
+                    d_pass(i, 0, c, t)
+        g_planes = d_planes[0][:, RAIN * S : (RAIN + 1) * S]
         for a in range(PASSES):
             move_planes(g_planes, got_slope, a, ROWS * a)
-        sig = [held([P, HALF], F32, f"sig{b}") for b in range(CHUNKS)]
-        for h in range(2):
-            for t in range(PACK):
-                w4_pass(1, h, t, second[SOIL, h][:])
-            for t in range(PACK):
-                w1_pass(1, h, t, second[RAIN, h][:])
-                nc.scalar.activation(sig[PACK * h + t][:], d_banks[PACK * h + t][:], ACT.Sigmoid, scale=-1.0)
+        sig = [placed([P, 2 * QUARTER], F32, f"sig{b}", 58 + 2 * b) for b in range(CHUNKS)]
+        for c in range(QUARTERS):
+            for i in (SOIL, RAIN):
+                for t in range(PACK):
+                    d_pass(i, 1, c, t)
+            for b in (2 * c, 2 * c + 1):
+                nc.scalar.activation(
+                    sig[b][:], d_banks[b][:].rearrange("p t j -> p (t j)"), ACT.Sigmoid, scale=-1.0
+                )
 
-        slope0 = placed([P, S], U32, "slope0", 72)
-        gather(slope0[:], tab_w[0][:].bitcast(U32), SLOPE, 0, S)
+        for a in range(PASSES):
+            gather_slope(a, 1, 32 + 2 * a)
 
-        w8_sc = deal_scales(nc.vector, w8_sc_raw, "w8_sc")
-
-        wr_bf = placed([P, N * PACK], BF16, "wr_bf", 62)
+        wr_bf = held([P, N * PACK], BF16, "wr_bf")
         nc.gpsimd.tensor_scalar(
             wr_bf[:].rearrange("p (s m t) -> p m s t", s=PACK, t=PACK),
             wr_raw[:].rearrange("p t (m s) -> p m s t", s=PACK),
@@ -238,14 +238,11 @@ def tile_list_runoff_routing_kernel(
             ALU.mult,
             ALU.add,
         )
-        wr_q = held([P, N], U32, "wr_q", "w1_bf0")
-        wr_sc = held([P, N], U8, "wr_sc")
-        nc.vector.quantize_mx(wr_q[:].bitcast(E4M3), wr_sc[:], wr_bf[:])
 
-        logs = placed([P, S * PACK], F32, "logs", 16)
+        logs = [placed([P, 2 * QUARTER], F32, f"logs{b}", 54 + 2 * b if b > 1 else (16.5, 49.5)[b]) for b in range(CHUNKS)]
         for b in range(CHUNKS):
-            nc.scalar.activation(logs[:, b * HALF : (b + 1) * HALF], sig[b][:], ACT.Ln, bias=floor[:])
-        soft = [placed([P, PACK, HALF], F32, f"soft{h}", 56 + 8 * h) for h in range(2)]
+            nc.scalar.activation(logs[b][:], sig[b][:], ACT.Ln, bias=floor[:])
+        soft = held([P, PACK * S], F32, "soft")
         y_q = held([P, S], U32, "y_q")
         y_sc = held([P, S], U8, "y_sc")
         y_bf = held([P, S * PACK], BF16, "y_bf")
@@ -255,24 +252,23 @@ def tile_list_runoff_routing_kernel(
 
         def softplus(b):
             nc.vector.scalar_tensor_tensor(
-                soft[b // PACK][:, b % PACK, :],
-                logs[:, b * HALF : (b + 1) * HALF],
+                soft[:, b * 2 * QUARTER : (b + 1) * 2 * QUARTER],
+                logs[b][:],
                 -1.0,
-                d_banks[b][:],
+                d_banks[b][:].rearrange("p t j -> p (t j)"),
                 ALU.mult,
                 ALU.max,
             )
-
-        def project_slope(b):
             cells = slice(b * CELLS, (b + 1) * CELLS)
-            g_banks[b] = psum.tile([P, PACK, CELLS], F32, name=f"g{b}", tag=f"bank{b % G_BANKS}")
+            mine = slice(b % PACK * CELLS, (b % PACK + 1) * CELLS)
+            g_banks[b] = psum.tile([P, PACK, CELLS], F32, name=f"g{b}", tag=f"bank{b}")
             for t in range(PACK):
-                for a, words in enumerate((slope0[:, cells], slope1[:, cells])):
+                for a in range(PASSES):
                     nc.tensor.matmul_mx(
                         g_banks[b][:, t, :],
                         lhsT=w8_q[:, a, t * P : (t + 1) * P].bitcast(E4M3),
                         lhsT_scale=w8_sc[:, a * H + t * P : a * H + (t + 1) * P],
-                        rhs=words.bitcast(E4M3),
+                        rhs=slope[a, b // PACK][:, mine].bitcast(E4M3),
                         rhs_scale=g_planes[ROWS * a :, cells],
                         start=a == 0,
                         stop=a == PASSES - 1,
@@ -280,7 +276,8 @@ def tile_list_runoff_routing_kernel(
 
         def product(c):
             h_bf[c] = ring.tile([P, CELLS * PACK], BF16, name="h_bf", align_bytes=64)
-            mine = soft[c // PACK][:, :, c % PACK * CELLS : (c % PACK + 1) * CELLS]
+            quarter = soft[:, c // 2 * PACK * QUARTER : (c // 2 + 1) * PACK * QUARTER]
+            mine = quarter.rearrange("p (t j) -> p t j", t=PACK)[:, :, c % 2 * CELLS : (c % 2 + 1) * CELLS]
             nc.vector.tensor_tensor(
                 h_bf[c][:].rearrange("p (j i t) -> p j t i", t=PACK, i=2),
                 g_banks[c][:].rearrange("p t (j i) -> p j t i", i=2),
@@ -292,8 +289,7 @@ def tile_list_runoff_routing_kernel(
             h_q = ring.tile([P, CELLS], U32, name="h_q", align_bytes=64)
             h_sc = ring.tile([P, CELLS], U8, name="h_sc", align_bytes=64)
             nc.vector.quantize_mx(h_q[:].bitcast(E4M3), h_sc[:], h_bf[c][:])
-            bank = c + G_BANKS if c + G_BANKS < CHUNKS else c % G_BANKS
-            y_banks[c] = psum.tile([P, PACK, CELLS], F32, name=f"y{c}", tag=f"bank{bank}")
+            y_banks[c] = psum.tile([P, PACK, CELLS], F32, name=f"y{c}", tag=f"bank{c}")
             for s in range(PACK):
                 nc.tensor.matmul_mx(
                     y_banks[c][:, s, :],
@@ -329,39 +325,34 @@ def tile_list_runoff_routing_kernel(
 
         def finish(c):
             route(c)
-            if c < PACK:
-                round_y(c, nc.scalar.copy)
             store_y(c)
-            if c >= PACK:
-                round_y(c, nc.scalar.copy)
+            round_y(c, nc.scalar.copy)
 
-        for b in range(PACK):
+        for b in range(3):
             softplus(b)
-            if b < G_BANKS:
-                project_slope(b)
-        for c in range(PACK):
+        product(0)
+        wr_q = placed([P, N], U32, "wr_q", 58)
+        wr_sc = held([P, N], U8, "wr_sc")
+        nc.vector.quantize_mx(wr_q[:].bitcast(E4M3), wr_sc[:], wr_bf[:])
+        finish(0)
+        softplus(3)
+        for c in range(1, 5):
             product(c)
-            project_slope(c + G_BANKS)
-            softplus(c + PACK)
+            softplus(c + 3)
             finish(c)
-        for c in range(PACK, CHUNKS - 2):
-            product(c)
-            if c + G_BANKS < CHUNKS:
-                project_slope(c + G_BANKS)
-            store_planes(c - PACK)
-            finish(c)
-        product(CHUNKS - 2)
-        product(CHUNKS - 1)
-        route(CHUNKS - 2)
-        store_y(CHUNKS - 2)
-        route(CHUNKS - 1)
+        product(5)
+        store_planes(0)
+        finish(5)
+        product(6)
+        store_planes(1)
+        route(6)
+        store_y(6)
+        product(7)
         store_planes(2)
-        round_y(CHUNKS - 1, nc.vector.tensor_copy)
-        store_y(CHUNKS - 1)
-        round_stored_y(CHUNKS - 2)
+        route(7)
+        round_stored_y(6)
+        round_y(7, nc.vector.tensor_copy)
+        store_y(7)
         store_planes(3)
-        for q in range(QUADS):
-            nc.sync.dma_start(
-                out_2[0, ROWS * q : ROWS * (q + 1), :].bitcast(I32),
-                y_sc[32 * q : 32 * q + ROWS, :].bitcast(I32),
-            )
+        for r in range(ROWS):
+            nc.sync.dma_start(out_2[0, r:16:ROWS, :].bitcast(I32), y_sc[r:P:32, :].bitcast(I32))

@@ -101,22 +101,22 @@ def tile_list_runoff_routing_kernel(
 
         move_planes(d_planes[0], got_sc, 0)
 
-        w4_q = held([P, PASSES, H // 2], I32, "w4_q")
-        nc.gpsimd.tensor_copy(
+        w4_q = held([P, PASSES, H // 2], U32, "w4_q")
+        nc.scalar.copy(
             w4_q[:].rearrange("p a (t q i) -> p a t q i", t=PACK, i=4),
-            w4_raw[:].rearrange("p a (q t i) -> p a t q i", t=PACK, i=4),
+            w4_raw[:].bitcast(U32).rearrange("p a (q t i) -> p a t q i", t=PACK, i=4),
         )
         w1_raw.append(placed([P, PACK, H], F32, "w1_raw1", 31))
         nc.sync.dma_start(w1_raw[1][:], w1_rows[1])
 
-        def deal_scales(engine, raw, dealt):
-            engine.tensor_copy(
-                dealt[:].bitcast(I32).rearrange("p (a t q i) -> p a t q i", a=PASSES, t=PACK, i=2),
-                raw.bitcast(I32).rearrange("p (a q t i) -> p a t q i", a=PASSES, t=PACK, i=2),
+        def deal_scales(copy, raw, dealt):
+            copy(
+                dealt[:].bitcast(U32).rearrange("p (a t q i) -> p a t q i", a=PASSES, t=PACK, i=2),
+                raw.bitcast(U32).rearrange("p (a q t i) -> p a t q i", a=PASSES, t=PACK, i=2),
             )
             return dealt
 
-        w4_sc = deal_scales(nc.gpsimd, w4_sc_raw[:], held([P, PASSES * H], U8, "w4_sc"))
+        w4_sc = deal_scales(nc.scalar.copy, w4_sc_raw[:], held([P, PASSES * H], U8, "w4_sc"))
         tab_w.append(placed([P, T], I32, "tab_w1", 0.5))
         load_table(tab_w[1], 1)
         d_planes.append(placed([P, 2 * S], U8, "d_planes1", 16.5))
@@ -183,7 +183,7 @@ def tile_list_runoff_routing_kernel(
             w8_q[:].rearrange("p a (t q i) -> p a t q i", t=PACK, i=8),
             w8_raw[:].rearrange("p a (q t i) -> p a t q i", t=PACK, i=8),
         )
-        w8_sc = deal_scales(nc.gpsimd, w8_sc_raw[:], held([P, PASSES * H], U8, "w8_sc"))
+        w8_sc = deal_scales(nc.gpsimd.tensor_copy, w8_sc_raw[:], held([P, PASSES * H], U8, "w8_sc"))
 
         d_banks = [psum.tile([P, 2, QUARTER], F32, name=f"d{b}", tag=f"bank{b}") for b in range(CHUNKS)]
 

@@ -229,7 +229,7 @@ def tile_list_runoff_routing_kernel(
         for a in range(PASSES):
             gather_slope(a, 1, 32 + 2 * a)
 
-        wr_bf = held([P, N * PACK], BF16, "wr_bf")
+        wr_bf = placed([P, N * PACK], BF16, "wr_bf", 80)
         nc.gpsimd.tensor_scalar(
             wr_bf[:].rearrange("p (s m t) -> p m s t", s=PACK, t=PACK),
             wr_raw[:].rearrange("p t (m s) -> p m s t", s=PACK),
@@ -238,11 +238,14 @@ def tile_list_runoff_routing_kernel(
             ALU.mult,
             ALU.add,
         )
+        wr_q = held([P, N], U32, "wr_q")
+        wr_sc = held([P, N], U8, "wr_sc")
+        nc.vector.quantize_mx(wr_q[:].bitcast(E4M3), wr_sc[:], wr_bf[:])
 
         logs = [placed([P, 2 * QUARTER], F32, f"logs{b}", 54 + 2 * b if b > 1 else (16.5, 49.5)[b]) for b in range(CHUNKS)]
         for b in range(CHUNKS):
             nc.scalar.activation(logs[b][:], sig[b][:], ACT.Ln, bias=floor[:])
-        soft = held([P, PACK * S], F32, "soft")
+        soft = placed([P, PACK * S], F32, "soft", 83)
         y_q = held([P, S], U32, "y_q")
         y_sc = held([P, S], U8, "y_sc")
         y_bf = held([P, S * PACK], BF16, "y_bf")
@@ -330,13 +333,7 @@ def tile_list_runoff_routing_kernel(
 
         for b in range(3):
             softplus(b)
-        product(0)
-        wr_q = placed([P, N], U32, "wr_q", 58)
-        wr_sc = held([P, N], U8, "wr_sc")
-        nc.vector.quantize_mx(wr_q[:].bitcast(E4M3), wr_sc[:], wr_bf[:])
-        finish(0)
-        softplus(3)
-        for c in range(1, 5):
+        for c in range(5):
             product(c)
             softplus(c + 3)
             finish(c)

@@ -125,7 +125,7 @@ def tile_list_runoff_routing_kernel(
 
         early = (S, S - QUARTER)
         first = [held([P, early[i]], U32, f"first{i}") for i in range(2)]
-        for i in (SOIL, RAIN):
+        for i in (RAIN, SOIL):
             gather(first[i][:], tab_w[0][:].bitcast(U32), i, 0, early[i])
         got_slope = placed([P, S], U8, "got_slope", 30)
         gather(got_slope[:], tab_sc[:], SLOPE, 0, S)

@@ -339,17 +339,19 @@ def tile_list_runoff_routing_kernel(
             finish(c)
         product(5)
         store_planes(0)
-        finish(5)
+        route(5)
+        store_y(5)
         product(6)
-        store_planes(1)
+        product(7)
         route(6)
         store_y(6)
-        product(7)
-        store_planes(2)
         route(7)
-        round_stored_y(6)
+        store_planes(1)
+        round_stored_y(5)
         round_y(7, nc.vector.tensor_copy)
         store_y(7)
+        store_planes(2)
+        round_stored_y(6)
         store_planes(3)
         for r in range(ROWS):
             nc.sync.dma_start(out_2[0, r:16:ROWS, :].bitcast(I32), y_sc[r:P:32, :].bitcast(I32))

from contextlib import ExitStack

import concourse.mybir as mybir

K, T, S, H, N = 1024, 4096, 1024, 512, 512
FLOPS = 2 * S * H * (3 * K + N)

F32 = mybir.dt.float32
BF16 = mybir.dt.bfloat16
I32 = mybir.dt.int32
U32 = mybir.dt.uint32
U16 = mybir.dt.uint16
U8 = mybir.dt.uint8
E4M3 = mybir.dt.float8_e4m3fn_x4
E2M1 = mybir.dt.float4_e2m1fn_x4
ACT = mybir.ActivationFunctionType
ALU = mybir.AluOpType

P = 128
PACK = 4
PASSES = K // (P * PACK)
ROWS = 4
CELLS = 128
CHUNKS = S // CELLS
QUARTERS = 4
QUARTER = S // QUARTERS
HALF = S // 2
LIMIT = 40.0
SOIL, RAIN, SLOPE = 0, 1, 2
KIB = 1024


def tile_list_runoff_routing_kernel(
    tc, tab_words, tab_scales, offs, offs2, offs3, w1, w4_words, w4_scales, w8_words, w8_scales, wr,
    out_0, out_1, out_2,
):
    nc = tc.nc
    with ExitStack() as ctx:
        keep = ctx.enter_context(tc.tile_pool(name="keep", bufs=1))
        ring = ctx.enter_context(tc.tile_pool(name="ring", bufs=4))
        shared = ctx.enter_context(tc.tile_pool(name="shared", bufs=1))
        psum = ctx.enter_context(tc.psum_pool(name="psum", bufs=1))

        def held(shape, dtype, name):
            return keep.tile(shape, dtype, name=name, tag=name, align_bytes=64)

        def placed(shape, dtype, name, kib):
            return shared.tile(shape, dtype, name=name, offset=int(kib * KIB), align_bytes=64)

        def zero(engine, ap):
            engine.memset(ap.bitcast(I32), 0)

        tab_sc = held([P, T], U8, "tab_sc")
        zero(nc.vector, tab_sc[64:P, :])
        zero(nc.vector, tab_sc[32:64, :])
        w4_sc_raw = placed([P, PASSES * H], U8, "w4_sc_raw", 16)
        zero(nc.gpsimd, w4_sc_raw[:])
        limit = held([P, 1], F32, "limit")
        nc.gpsimd.memset(limit[:], -LIMIT)
        floor = held([P, 1], F32, "floor")
        nc.scalar.activation(floor[:], limit[:], ACT.Sigmoid)
        d_planes = [held([P, 2 * S], U8, "d_planes0")]
        zero(nc.gpsimd, d_planes[0][:])

        lists = [held([P, S // 16], U16, f"list{i}") for i in range(3)]
        nc.sync.dma_start(tab_sc[0:32, :].bitcast(I32), tab_scales.rearrange("a q t -> (a q) t").bitcast(I32))
        for tile, src in zip(lists, (offs2, offs, offs3)):
            nc.sync.dma_start(tile[:], src)

        def load_table(tile, a):
            nc.sync.dma_start(tile[:], tab_words[a].rearrange("p n i -> p (n i)").bitcast(I32))

        def load_scale_rows(tile, src):
            for r in range(ROWS):
                nc.sync.dma_start(
                    tile[r:P:32, :].bitcast(I32).rearrange("q (a c) -> q a c", a=PASSES),
                    src[:, r:16:ROWS, :].bitcast(I32).rearrange("a q c -> q a c"),
                )

        w1_rows = w1.rearrange("(a p j) c -> a p j c", a=PASSES, j=PACK)
        tab_w = [held([P, T], I32, "tab_w0")]
        load_table(tab_w[0], 0)
        w4_raw = placed([P, PASSES, H // 2], I32, "w4_raw", 30)
        nc.sync.dma_start(w4_raw[:], w4_words.bitcast(I32).rearrange("a p c -> p a c"))
        load_scale_rows(w4_sc_raw, w4_scales)
        w1_raw = [placed([P, PACK, H], F32, "w1_raw0", 20)]
        nc.sync.dma_start(w1_raw[0][:], w1_rows[0])

        def gather(out, window, which, lo, hi):
            nc.vector.tensor_copy(out, window.indirect(lists[which][:, lo // 16 : hi // 16]))

        got_sc = held([P, 2 * S], U8, "got_sc")
        for i in (SOIL, RAIN):
            gather(got_sc[:, i * S : (i + 1) * S], tab_sc[:], i, 0, S)

        def move_planes(dst, src, a, row=0):
            for r in range(ROWS):
                nc.sync.dma_start(
                    dst[row + r : P : 32, :].bitcast(I32), src[16 * a + r : 16 * (a + 1) : ROWS, :].bitcast(I32)
                )

        move_planes(d_planes[0], got_sc, 0)

        w4_q = held([P, PASSES, H // 2], U32, "w4_q")
        nc.scalar.copy(
            w4_q[:].rearrange("p a (t q i) -> p a t q i", t=PACK, i=4),
            w4_raw[:].bitcast(U32).rearrange("p a (q t i) -> p a t q i", t=PACK, i=4),
        )
        w1_raw.append(placed([P, PACK, H], F32, "w1_raw1", 31))
        nc.sync.dma_start(w1_raw[1][:], w1_rows[1])

        def deal_scales(copy, raw, dealt):
            copy(
                dealt[:].bitcast(U32).rearrange("p (a t q i) -> p a t q i", a=PASSES, t=PACK, i=2),
                raw.bitcast(U32).rearrange("p (a q t i) -> p a t q i", a=PASSES, t=PACK, i=2),
            )
            return dealt

        w4_sc = deal_scales(nc.scalar.copy, w4_sc_raw[:], held([P, PASSES * H], U8, "w4_sc"))
        tab_w.append(placed([P, T], I32, "tab_w1", 0.5))
        load_table(tab_w[1], 1)
        d_planes.append(placed([P, 2 * S], U8, "d_planes1", 16.5))
        zero(nc.gpsimd, d_planes[1][:])
        move_planes(d_planes[1], got_sc, 1)

        early = (S, S - QUARTER)
        first = [held([P, early[i]], U32, f"first{i}") for i in range(2)]
        for i in (RAIN, SOIL):
            gather(first[i][:], tab_w[0][:].bitcast(U32), i, 0, early[i])
        got_slope = placed([P, S], U8, "got_slope", 30)
        gather(got_slope[:], tab_sc[:], SLOPE, 0, S)
        w1_q = [held([P, H], U32, f"w1_q{a}") for a in range(PASSES)]
        w1_sc = [held([P, H], U8, f"w1_sc{a}") for a in range(PASSES)]

        def quantise_w1(a):
            w1_bf = placed([P, H * PACK], BF16, f"w1_bf{a}", 76 - 28 * a)
            dst = w1_bf[:].rearrange("p (t q u i j) -> p u t q j i", t=PACK, u=2, i=4, j=PACK)
            src = w1_raw[a][:].rearrange("p j (q t u i) -> p u t q j i", t=PACK, u=2, i=4)
            for u in range(2):
                nc.scalar.copy(dst[:, u, : PACK - 1], src[:, u, : PACK - 1])
            nc.gpsimd.tensor_scalar(
                w1_bf[:].rearrange("p (t q i j) -> p t q j i", t=PACK, i=8, j=PACK)[:, PACK - 1],
                w1_raw[a][:].rearrange("p j (q t i) -> p t q j i", t=PACK, i=8)[:, PACK - 1],
                1.0,
                0.0,
                ALU.mult,
                ALU.add,
            )
            nc.vector.quantize_mx(w1_q[a][:].bitcast(E4M3), w1_sc[a][:], w1_bf[:])

        quantise_w1(0)
        slope = {}

        def gather_slope(a, h, kib):
            slope[a, h] = placed([P, HALF], U32, f"slope{a}{h}", kib)
            gather(slope[a, h][:], tab_w[a][:].bitcast(U32), SLOPE, h * HALF, (h + 1) * HALF)

        gather_slope(0, 0, 25)
        quantise_w1(1)
        first_tail = placed([P, QUARTER], U32, "first_tail", 50.5)
        gather(first_tail[:], tab_w[0][:].bitcast(U32), RAIN, early[RAIN], S)

        w8_raw = placed([P, PASSES, H], I32, "w8_raw", 20)
        nc.sync.dma_start(
            w8_raw[:], w8_words.rearrange("a p c i -> a p (c i)").bitcast(I32).rearrange("a p c -> p a c")
        )
        w8_sc_raw = placed([P, PASSES * H], U8, "w8_sc_raw", 24)
        zero(nc.gpsimd, w8_sc_raw[:])
        load_scale_rows(w8_sc_raw, w8_scales)
        wr_raw = placed([P, PACK, N], F32, "wr_raw", 38.5)
        wr_rows = wr.rearrange("(q t i) n -> t q i n", t=PACK, i=8)
        for t in range(PACK):
            nc.sync.dma_start(wr_raw[:, t, :], wr_rows[t])

        second = {}
        for c in range(QUARTERS):
            for i in (SOIL, RAIN):
                second[i, c] = placed([P, QUARTER], U32, f"second{i}{c}", (32 if c < 3 else 42.5) + 2 * c + i)
                gather(second[i, c][:], tab_w[1][:].bitcast(U32), i, c * QUARTER, (c + 1) * QUARTER)
        gather_slope(1, 0, 51.5)
        w8_q = held([P, PASSES, H], I32, "w8_q")
        nc.gpsimd.tensor_copy(
            w8_q[:].rearrange("p a (t q i) -> p a t q i", t=PACK, i=8),
            w8_raw[:].rearrange("p a (q t i) -> p a t q i", t=PACK, i=8),
        )
        w8_sc = deal_scales(nc.gpsimd.tensor_copy, w8_sc_raw[:], held([P, PASSES * H], U8, "w8_sc"))

        d_banks = [psum.tile([P, 2, QUARTER], F32, name=f"d{b}", tag=f"bank{b}") for b in range(CHUNKS)]

        def d_pass(i, a, c, t):
            cells = slice(c * QUARTER, (c + 1) * QUARTER)
            if a == 1:
                words = second[i, c][:]
            else:
                words = first[i][:, cells] if cells.stop <= early[i] else first_tail[:]
            if i == SOIL:
                lhsT = w4_q[:, a, t * P // 2 : (t + 1) * P // 2].bitcast(U8).bitcast(E2M1)
                lhsT_scale = w4_sc[:, a * H + t * P : a * H + (t + 1) * P]
            else:
                lhsT = w1_q[a][:, t * P : (t + 1) * P].bitcast(E4M3)
                lhsT_scale = w1_sc[a][:, t * P : (t + 1) * P]
            nc.tensor.matmul_mx(
                d_banks[2 * c + t // 2][:, t % 2, :],
                lhsT=lhsT,
                lhsT_scale=lhsT_scale,
                rhs=words.bitcast(E4M3),
                rhs_scale=d_planes[a][:, i * S + c * QUARTER : i * S + (c + 1) * QUARTER],
                start=(i, a, t % 2) == (SOIL, 0, 0),
                stop=(i, a, t % 2) == (RAIN, PASSES - 1, 1),
            )

        for i in (SOIL, RAIN):
            for c in range(QUARTERS):
                for t in range(PACK):
                    d_pass(i, 0, c, t)
        g_planes = d_planes[0][:, RAIN * S : (RAIN + 1) * S]
        for a in range(PASSES):
            move_planes(g_planes, got_slope, a, ROWS * a)
        sig = [placed([P, 2 * QUARTER], F32, f"sig{b}", 58 + 2 * b) for b in range(CHUNKS)]
        for c in range(QUARTERS):
            for i in (SOIL, RAIN):
                for t in range(PACK):
                    d_pass(i, 1, c, t)
            for b in (2 * c, 2 * c + 1):
                nc.scalar.activation(
                    sig[b][:], d_banks[b][:].rearrange("p t j -> p (t j)"), ACT.Sigmoid, scale=-1.0
                )

        for a in range(PASSES):
            gather_slope(a, 1, 32 + 2 * a)

        wr_bf = placed([P, N * PACK], BF16, "wr_bf", 80)
        nc.gpsimd.tensor_scalar(
            wr_bf[:].rearrange("p (s m t) -> p m s t", s=PACK, t=PACK),
            wr_raw[:].rearrange("p t (m s) -> p m s t", s=PACK),
            1.0,
            0.0,
            ALU.mult,
            ALU.add,
        )
        wr_q = held([P, N], U32, "wr_q")
        wr_sc = held([P, N], U8, "wr_sc")
        nc.vector.quantize_mx(wr_q[:].bitcast(E4M3), wr_sc[:], wr_bf[:])

        logs = [placed([P, 2 * QUARTER], F32, f"logs{b}", 54 + 2 * b if b > 1 else (16.5, 49.5)[b]) for b in range(CHUNKS)]
        for b in range(CHUNKS):
            nc.scalar.activation(logs[b][:], sig[b][:], ACT.Ln, bias=floor[:])
        soft = placed([P, PACK * S], F32, "soft", 83)
        y_q = held([P, S], U32, "y_q")
        y_sc = held([P, S], U8, "y_sc")
        y_bf = held([P, S * PACK], BF16, "y_bf")
        y_rows = out_0.rearrange("(p t) j -> p t j", t=PACK)
        y_words = out_1[0].rearrange("p m t -> p (m t)").bitcast(I32)
        g_banks, h_bf, y_banks, y_sb = {}, {}, {}, {}

        def softplus(b):
            nc.vector.scalar_tensor_tensor(
                soft[:, b * 2 * QUARTER : (b + 1) * 2 * QUARTER],
                logs[b][:],
                -1.0,
                d_banks[b][:].rearrange("p t j -> p (t j)"),
                ALU.mult,
                ALU.max,
            )
            cells = slice(b * CELLS, (b + 1) * CELLS)
            mine = slice(b % PACK * CELLS, (b % PACK + 1) * CELLS)
            g_banks[b] = psum.tile([P, PACK, CELLS], F32, name=f"g{b}", tag=f"bank{b}")
            for t in range(PACK):
                for a in range(PASSES):
                    nc.tensor.matmul_mx(
                        g_banks[b][:, t, :],
                        lhsT=w8_q[:, a, t * P : (t + 1) * P].bitcast(E4M3),
                        lhsT_scale=w8_sc[:, a * H + t * P : a * H + (t + 1) * P],
                        rhs=slope[a, b // PACK][:, mine].bitcast(E4M3),
                        rhs_scale=g_planes[ROWS * a :, cells],
                        start=a == 0,
                        stop=a == PASSES - 1,
                    )

        def product(c):
            h_bf[c] = ring.tile([P, CELLS * PACK], BF16, name="h_bf", align_bytes=64)
            quarter = soft[:, c // 2 * PACK * QUARTER : (c // 2 + 1) * PACK * QUARTER]
            mine = quarter.rearrange("p (t j) -> p t j", t=PACK)[:, :, c % 2 * CELLS : (c % 2 + 1) * CELLS]
            nc.vector.tensor_tensor(
                h_bf[c][:].rearrange("p (j i t) -> p j t i", t=PACK, i=2),
                g_banks[c][:].rearrange("p t (j i) -> p j t i", i=2),
                mine.rearrange("p t (j i) -> p j t i", i=2),
                ALU.mult,
            )

        def route(c):
            h_q = ring.tile([P, CELLS], U32, name="h_q", align_bytes=64)
            h_sc = ring.tile([P, CELLS], U8, name="h_sc", align_bytes=64)
            nc.vector.quantize_mx(h_q[:].bitcast(E4M3), h_sc[:], h_bf[c][:])
            y_banks[c] = psum.tile([P, PACK, CELLS], F32, name=f"y{c}", tag=f"bank{c}")
            for s in range(PACK):
                nc.tensor.matmul_mx(
                    y_banks[c][:, s, :],
                    lhsT=wr_q[:, s * P : (s + 1) * P].bitcast(E4M3),
                    lhsT_scale=wr_sc[:, s * P : (s + 1) * P],
                    rhs=h_q[:].bitcast(E4M3),
                    rhs_scale=h_sc[:],
                    start=True,
                    stop=True,
                )

        def round_y(c, copy):
            rounded = y_bf[:, c * PACK * CELLS : (c + 1) * PACK * CELLS]
            copy(rounded.rearrange("p (j s) -> p j s", s=PACK), y_banks[c][:].rearrange("p s j -> p j s"))

        def store_y(c):
            y_sb[c] = held([P, PACK, CELLS], F32, f"y_sb{c}")
            nc.scalar.copy(y_sb[c][:], y_banks[c][:])
            nc.sync.dma_start(y_rows[:, :, c * CELLS : (c + 1) * CELLS], y_sb[c][:])

        def store_planes(k):
            pair = slice(2 * k * CELLS, 2 * (k + 1) * CELLS)
            wide = slice(2 * k * PACK * CELLS, 2 * (k + 1) * PACK * CELLS)
            nc.vector.quantize_mx(y_q[:, pair].bitcast(E4M3), y_sc[:, pair], y_bf[:, wide])
            nc.sync.dma_start(y_words[:, pair], y_q[:, pair].bitcast(I32))

        def round_stored_y(c):
            rounded = y_bf[:, c * PACK * CELLS : (c + 1) * PACK * CELLS]
            nc.vector.tensor_copy(
                rounded.rearrange("p (j i s) -> p j s i", s=PACK, i=4),
                y_sb[c][:].rearrange("p s (j i) -> p j s i", i=4),
            )

        def finish(c):
            route(c)
            store_y(c)
            round_y(c, nc.scalar.copy)

        for b in range(3):
            softplus(b)
        for c in range(5):
            product(c)
            softplus(c + 3)
            finish(c)
        product(5)
        store_planes(0)
        route(5)
        store_y(5)
        product(6)
        product(7)
        route(6)
        store_y(6)
        route(7)
        store_planes(1)
        round_stored_y(5)
        round_y(7, nc.vector.tensor_copy)
        store_y(7)
        store_planes(2)
        round_stored_y(6)
        store_planes(3)
        for r in range(ROWS):
            nc.sync.dma_start(out_2[0, r:16:ROWS, :].bitcast(I32), y_sc[r:P:32, :].bitcast(I32))
